import numpy as np, ml_dtypes
CORES = [3,11,19,27,35,43,51,59]
N = 8
import mx_ref
BF = ml_dtypes.bfloat16
def cols(t, e):
    v = np.concatenate([t.reshape(128, -1, 4), np.zeros((128, 1, 4), BF)], axis=1)
    return np.ascontiguousarray(v[:, e]).reshape(128, -1)
def cut(t, i, w=512):
    return t[:, w * i:w * i + w]
def pick(q, e):
    c = np.concatenate([q[0].reshape(128, -1, 4), np.zeros((128, 1, 4), np.uint8)], axis=1); s = np.concatenate([q[1], np.ones((16, 1), np.uint8)], axis=1)
    return (np.ascontiguousarray(c[:, e].reshape(128, -1)), np.ascontiguousarray(s[:, e]))
def join(*qs):
    return (np.concatenate([q[0] for q in qs], axis=1), np.concatenate([q[1] for q in qs], axis=1))
def put(q, e, v):
    c, s = q[0].reshape(128, -1, 4).copy(), q[1].copy(); c[:, e] = v[0].reshape(128, -1, 4); s[:, e] = v[1]
    return (c.reshape(128, -1), s)
def pk(c, s):
    return (np.ascontiguousarray(c), mx_ref.live(s))
def emit(q):
    return q[0], q[1]
def decode(q):
    o = []
    for b in range(4):
        e = np.zeros((128, 128, 4), np.float32); e[np.arange(128), np.arange(128), b] = 1
        o.append(mx_ref.matmul(mx_ref.quantize(e.reshape(128, 512).astype(BF)), q))
    return np.stack(o, axis=2).reshape(128, -1)
def f(rng, *shape):
    return mx_ref.flush((rng.standard_normal(shape, dtype=np.float32) * np.exp2(rng.integers(-2, 3, shape[:-1] + (1,)))).astype(BF))
def wide(rng, *shape, cols=0):
    v = rng.standard_normal(shape, dtype=np.float32) * np.exp2(rng.integers(-12, 13, shape)).astype(np.float32)
    if cols: v *= np.repeat(np.exp2(rng.integers(-cols, cols + 1, shape[:-2] + (1, shape[-1] // 4))) * (rng.random(shape[:-2] + (1, shape[-1] // 4)) > 0.0625), 4, axis=-1).astype(np.float32)
    return mx_ref.flush(v.astype(BF))
C, R, O = 256, 2, 1
def sized(v, k=1):
    v = np.asarray(v).astype(np.float32) * np.asarray(k, np.float32)
    v[np.abs(v) < np.float32(2.0 ** -8)] = 0
    return v.astype(BF)
def alike(t):
    return np.repeat(t[None], N, axis=0)
def setup_inputs(rng):
    k = np.exp2(rng.integers(1, 6, (N, 1, C)))
    return {"x": sized(f(rng, N, 128, 4 * C), np.repeat(k, 4, axis=2)), "b": alike(sized(f(rng, 128, 512), 8)), "w": f(rng, N, 128, 512 * O)}
def setup_inputs_ties(rng):
    d = setup_inputs(rng)
    x = np.stack([cols(d["x"][r], rng.permutation(C) % 24 - 1) for r in range(N)])
    z, e = int(rng.integers(0, N)), np.full(C, -1)
    e[int(rng.integers(0, C))] = 0
    x[z] = cols(d["x"][z], e)
    return {"x": x, "b": alike(cols(d["b"][0], rng.permutation(128) % 12 - 1)), "w": d["w"]}
def setup_inputs_near(rng):
    p = rng.choice([-1.0, 1.0], (128, 64, 4))
    k = np.sort(rng.permutation(128).reshape(64, 2), axis=1)
    b = np.zeros((128, 128, 4))
    b[:, k[:, 0]] = p
    b[:, k[:, 1]] = p
    b[:8] = 0
    b[120:] = 0
    b[127, k[:, 1], 3] = 1
    x = np.zeros((N, 128, C, 4))
    for r in range(N):
        v = 0.5 * rng.choice([-1.0, 1.0], (128, C, 4))
        j = np.sort(rng.permutation(C)[:128].reshape(64, 2), axis=1)
        v[:, j[:, 0]] = p
        v[:, j[:, 1]] = p
        v[120:] = 0
        v[127, j[:, 1], 3] = 2.0 ** -14
        x[r] = v * 2.0 ** int(rng.integers(8, 12))
    x[0, :8] = 2.0 ** 27
    x[1:N - 1, :8] = rng.choice([-1.0, 1.0], (N - 2, 8, C, 4)) * rng.integers(1, 16, (N - 2, 8, C, 4))
    x[N - 1, :8] = -2.0 ** 27
    return {"x": sized(x.reshape(N, 128, 4 * C)), "b": alike(sized(b.reshape(128, 512))), "w": f(rng, N, 128, 512 * O)}
def setup_inputs_low(rng):
    sign = np.ones(N)
    sign[rng.permutation(N)[:N // 4]] = -1
    def far(*shape):
        return (1 + rng.random(shape)) * np.exp2(rng.integers(28, 30, shape))
    return {"x": sized(far(N, 128, 4 * C), sign[:, None, None]), "b": alike(sized(far(128, 512), -1)), "w": f(rng, N, 128, 512 * O)}
def setup_inputs_lone(rng):
    q = rng.choice([-1.0, 1.0], (128, C, 4)) * rng.integers(4, 8, (128, C, 4))
    h = int(rng.integers(0, N))
    x = np.stack([q[:, rng.permutation(C)] * (16.0 if r == h else 1.0) for r in range(N)])
    b = sized(f(rng, 128, 4), 8).astype(np.float32)[:, None, :] * np.exp2(rng.integers(0, 6, (1, 128, 1)))
    return {"x": sized(x.reshape(N, 128, 4 * C)), "b": alike(sized(b.reshape(128, 512))), "w": f(rng, N, 128, 512 * O)}
def setup_inputs_spread(rng):
    return {"x": sized(wide(rng, N, 128, 4 * C, cols=6), 64), "b": alike(sized(wide(rng, 128, 512, cols=4), 64)), "w": f(rng, N, 128, 512 * O)}
def check_inputs(d):
    bad = []
    for k, low in (("x", 2.0 ** -8), ("b", 2.0 ** -30), ("w", 2.0 ** -30)):
        v = np.abs(d[k].astype(np.float32))
        if not (np.isfinite(v).all() and ((v == 0) | (v >= low) & (v <= 2.0 ** 30)).all()): bad.append("a value of " + k)
    v = d["b"].astype(np.float32)
    if (v != v[:1]).any(): bad.append("b differs between ranks")
    return bad
def match(g):
    g = g + np.float32(0)
    j, k = np.argmax(g, axis=1), np.argmax(g, axis=0)
    both = k[j] == np.arange(128)
    e = j.copy()
    e[~both] = np.setdiff1d(np.arange(C), j[both])[:np.sum(~both)]
    return e, both
def reference(x, b, w):
    T = [mx_ref.quantize(np.ascontiguousarray(x[r])) for r in range(N)]
    B = mx_ref.quantize(np.ascontiguousarray(b[0]))
    pa = np.zeros((N, R, 128), np.float32)
    for t in range(R):
        m = [match(mx_ref.matmul(B, T[r])) for r in range(N)]
        v = [decode(pick(T[r], m[r][0])) for r in range(N)]
        s = v[0]
        for r in range(1, N): s = s + v[r]
        B = mx_ref.quantize((s * np.float32(0.125)).astype(BF))
        d = decode(B)
        for r in range(N):
            e, both = m[r]
            pa[r, t] = e
            new = mx_ref.quantize(((v[r] + d) * np.float32(0.5)).astype(BF))
            T[r] = put(T[r], e[both], pick(new, np.flatnonzero(both)))
    y = np.zeros((N, 128, O * (C + 128)), np.float32)
    oc, osc = np.zeros((N, 128, 4 * C), np.uint8), np.zeros((N, 16, C), np.uint8)
    for r in range(N):
        for o in range(O):
            i = o * (C + 128)
            y[r, :, i:i + C + 128] = mx_ref.matmul(mx_ref.quantize(np.ascontiguousarray(cut(w[r], o))), join(T[r], B))
        oc[r], osc[r] = emit(T[r])
    return {"y": y, "oc": oc, "osc": osc, "pa": pa}

@@ -1,0 +1,394 @@
+from concourse.bass import DstId, RemoteDMATransfer
+from concourse.mybir import dt, AluOpType, AxisListType, ActivationFunctionType
+
+R_, C_, K_, H_ = 2, 256, 128, 64
+NR = 8
+STEP, DROP, BIG = 512.0, 16384.0, 512.0
+
+SCRATCH = {}
+
+
+def _sb(name, n, dtype):
+    SCRATCH[name] = ("sbuf", [128, n], dtype)
+
+
+def _mx(name, n):
+    _sb(name + "q", n, "float8_e4m3fn_x4")
+    _sb(name + "s", n, "uint8")
+
+
+for _n, _w in (("xt", 1024), ("bt", 512), ("wt", 512), ("Et", 2048), ("Ct", 2048), ("Ft", 512), ("Mt", 512),
+               ("Ut", 512), ("Kt", 1024), ("At", 768), ("Vt", 512), ("dI", 128), ("iJ", 256), ("i16", 128),
+               ("zer", 256), ("junk", 256), ("F2", 256), ("qq", 128), ("key", 128)):
+    _sb(_n, _w, "bfloat16")
+for _n, _w in (("R", 256), ("RT", 256), ("Am", 128), ("A0", 128), ("D", 256), ("cols", 16), ("jc", 2), ("acc", 128),
+               ("ysb", 384), ("par", 256), ("c16", 16), ("j16", 16), ("z16", 16), ("u16", 16), ("v16", 16),
+               ("w16", 16)):
+    _sb(_n, _w, "float32")
+_sb("pint", 8, "int32")
+for _n, _w in (("E", 512), ("C", 512), ("Bb", 128), ("Tb", 256), ("Ww", 128), ("F", 128), ("M", 128), ("U", 128),
+               ("K", 256)):
+    _mx(_n, _w)
+for _t in range(R_):
+    _sb("offa%d" % _t, 8, "uint16")
+    _sb("offb%d" % _t, 16, "uint16")
+    for _n, _w in (("P", 128), ("L", 576), ("A", 128), ("B", 256), ("W", 384), ("T", 256)):
+        _mx("%s%d" % (_n, _t), _w)
+for _i in range(8):
+    SCRATCH["ps%d" % _i] = ("psum", [128, 512], "float32")
+
+SEMAPHORES = ["cv", "ca", "ct", "cg", "ldx", "ldb", "ldw", "out", "sent", "p0", "p1", "b0", "b1"]
+
+
+def _planes(T, topo):
+    groups = []
+    for r, c in enumerate(T.cores):
+        for gr in groups:
+            if topo.same_plane(topo.chip(T.cores[gr[0]]), topo.chip(c)):
+                gr.append(r)
+                break
+        else:
+            groups.append([r])
+    return groups
+
+
+def rank_program(g, core, T, topo):
+    rank = T.rank_of(core)
+    if rank is None:
+        return
+    A = AluOpType
+    F = ActivationFunctionType
+    V, S, PE = g.vector, g.scalar, g.tensor
+    queue = {"v": V, "a": S, "t": PE, "g": g, "s": g.sync}
+    csem = {"v": "cv", "a": "ca", "t": "ct", "g": "cg"}
+    total = {n: 0 for n in SEMAPHORES}
+    known = {q: {} for q in queue}
+    lastw, readers = {}, {}
+
+    def need(q, evs):
+        want = {}
+        for ev in evs:
+            if ev[3] == "t" and q == "t":
+                continue
+            if known[q].get(ev[0], 0) < ev[1] and (ev[0] not in want or want[ev[0]][1] < ev[1]):
+                want[ev[0]] = ev
+        for ev in sorted(want.values(), key=lambda e: e[3] == q):
+            if known[q].get(ev[0], 0) >= ev[1]:
+                continue
+            queue[q].wait_ge(T.sem[ev[0]], ev[1])
+            known[q][ev[0]] = ev[1]
+            for s, n in ev[2].items():
+                if known[q].get(s, 0) < n:
+                    known[q][s] = n
+
+    def deps(q, rd, wr):
+        evs = []
+        for k in rd:
+            if k in lastw:
+                evs.append(lastw[k])
+            if k.startswith("ps"):
+                evs += [e for e in readers.get(k, []) if e[3] != q]
+        for k in wr:
+            if k in lastw:
+                evs.append(lastw[k])
+            evs += readers.get(k, [])
+        need(q, evs)
+
+    def note(ev, rd, wr):
+        for k in rd:
+            readers.setdefault(k, []).append(ev)
+        for k in wr:
+            lastw[k] = ev
+            readers[k] = []
+
+    def op(q, fn, rd, wr):
+        deps(q, rd, wr)
+        s = csem[q]
+        total[s] += 1
+        fn().then_inc(T.sem[s], 1)
+        note((s, total[s], dict(known[q]), q), rd, wr)
+
+    def dma(q, out, in_, sem, rd, wr):
+        deps(q, rd, wr)
+        total[sem] += 16
+        queue[q].dma_start(out, in_).then_inc(T.sem[sem], 16)
+        note((sem, total[sem], dict(known[q]), "dma"), [], wr)
+
+    def arrives(sem, n, keys):
+        total[sem] = n
+        for k in keys:
+            lastw[k] = (sem, n, {}, "far")
+
+    def quant(name, a, b, tile, rd, wr):
+        op("v", lambda: V.quantize_mx(T[name + "q"][:, a:b], T[name + "s"][:, a:b], tile), rd, wr)
+
+    def mm(bank, n, w, wa, x, xa, rd, start=True, stop=True):
+        op("t", lambda: PE.matmul_mx(T["ps%d" % bank][:, 0:n], T[w + "q"][:, wa:wa + 128], T[w + "s"][:, wa:wa + 128],
+                                     T[x + "q"][:, xa:xa + n], T[x + "s"][:, xa:xa + n], start, stop),
+           rd, ["ps%d" % bank])
+
+    def pick(dst, da, src, sn, off, oa, ob, rd, key):
+        n = 16 * (ob - oa)
+        op("v", lambda: V.tensor_copy(T[dst + "q"][:, da:da + n].bitcast(dt.uint32),
+                                      T[src + "q"][:, 0:sn].bitcast(dt.uint32).indirect(T[off][:, oa:ob])),
+           [k + "q" for k in rd] + [off], [key + "q"])
+        op("a", lambda: S.activation(T[dst + "s"][:, da:da + n], T[src + "s"][:, 0:sn].indirect(T[off][:, oa:ob]),
+                                     F.Copy),
+           [k + "s" for k in rd] + [off], [key + "s"])
+
+    def ts(out, in0, s1, s2, op0, op1, rd, wr):
+        if op1 is None:
+            op("v", lambda: V.tensor_scalar(out, in0, s1, None, op0), rd, wr)
+        else:
+            op("v", lambda: V.tensor_scalar(out, in0, s1, s2, op0, op1), rd, wr)
+
+    def fill(ap, val, wr):
+        op("v", lambda: V.memset(ap, val), [], wr)
+
+    def iota(ap, pattern, base, cm, wr, small=True):
+        if small:
+            op("g", lambda: g.iota(ap, pattern, base, cm, allow_small_or_imprecise_dtypes=True), [], wr)
+        else:
+            op("g", lambda: g.iota(ap, pattern, base, cm), [], wr)
+
+    def send(parts, sem, rd):
+        deps("g", rd, [])
+        trs = []
+        for src, dsts, eng in parts:
+            ids = []
+            for r, _ in dsts:
+                rid, pid, _e = topo.addr(T.cores[r])
+                ids.append(DstId(rid=rid, pnc=pid))
+            trs.append(RemoteDMATransfer(dst_ids=ids, dma_engine_mask=sum(1 << e for e in eng),
+                                         remote_sem=T.sem[sem], src=src, dsts=[d for _, d in dsts]))
+            total["sent"] += len(eng)
+        g.remote_dma_fused(trs, local_sem=T.sem.sent)
+
+    def col(i):
+        return T.cols[:, i:i + 1]
+    JB, KB, CC, MU, PM, CORR = 0, 1, 3, 5, 7, 8
+
+    groups = _planes(T, topo)
+    mine = [gr for gr in groups if rank in gr][0]
+    eng = [e for e in range(16) if all(e in topo.engines(core, c) for c in T.cores if c != core)]
+    halves = [eng[:len(eng) // 2], eng[len(eng) // 2:]]
+
+    dma("s", T.xt[:], T.x[:], "ldx", [], ["xt"])
+    dma("a", T.bt[:], T.b[:], "ldb", [], ["bt"])
+    dma("s", T.wt[:], T.w[:], "ldw", ["xt"], ["wt"])
+
+    iota(T.dI[:], [[1, 128]], 0, -1, ["dI"])
+    iota(T.Ct[:, 0:512], [[0, 128], [-2, 2], [0, 2]], 1, 0, ["C0"])
+    iota(T.iJ[:], [[1, 256]], 0, 0, ["iJ"])
+    iota(T.pint[:, 0:1], [[0, 1]], 0, 1, ["pi0"], small=False)
+    iota(T.i16[:], [[0, 8], [1, 16]], 0, 0, ["i16"])
+    iota(T.jc[:], [[128, 2]], 1, 1, ["jc"])
+    iota(T.c16[:], [[16, 16]], 0, 0, ["c16"])
+
+    def make_e(lo):
+        for b in (lo, lo + 1):
+            ts(T.Et[:, 512 * b + b:512 * (b + 1):4], T.dI[:], 0.0, 0.125, A.is_equal, A.mult,
+               ["dI", "Ez%d" % lo], ["Et%d" % b])
+        quant("E", 128 * lo, 128 * lo + 256, T.Et[:, 512 * lo:512 * lo + 1024],
+              ["Et%d" % lo, "Et%d" % (lo + 1)], ["E%d" % lo, "E%d" % (lo + 1)])
+
+    fill(T.Ct[:, 512:1024], BIG, ["C1"])
+    fill(T.Et[:, 0:1024], 0.0, ["Ez0"])
+    fill(T.zer[:], 0.0, ["zer"])
+    fill(T.Ft[:], 0.0, ["Fz"])
+    fill(T.Mt[:], 0.0, ["Mz"])
+    op("a", lambda: S.activation(T.Ct[:, 1024:1536], T.Ct[:, 512:1024], F.Copy, scale=0.0), ["C1"], ["C2z"])
+    op("a", lambda: S.activation(T.Ct[:, 1536:2048], T.Ct[:, 512:1024], F.Copy, scale=1.0 / BIG), ["C1"], ["C3z"])
+    make_e(0)
+    ts(T.Ct[:, 1024:1536:4], T.dI[:], 0.0, None, A.is_ge, None, ["dI", "C2z"], ["C2"])
+    ts(T.Ct[:, 1537:2048:4], T.dI[:], 0.0, None, A.is_ge, None, ["dI", "C3z"], ["C3"])
+    quant("C", 0, 512, T.Ct[:], ["C0", "C1", "C2", "C3"], ["C"])
+    ts(T.pint[:, 4:5], T.pint[:, 0:1], 15, None, A.bitwise_and, None, ["pi0"], ["pi1"])
+    op("v", lambda: V.tensor_copy(col(PM), T.pint[:, 4:5]), ["pi1"], ["pm"])
+    ts(T.A0[:], T.i16[:], col(PM), DROP + STEP, A.not_equal, A.mult, ["i16", "pm"], ["A0"])
+    ts(col(CORR), col(PM), -STEP, 15 * STEP, A.mult, A.add, ["pm"], ["corr"])
+    op("a", lambda: S.activation(T.Am[:], T.A0[:], F.Identity, bias=-DROP), ["A0"], ["Am"])
+
+    quant("Bb", 0, 128, T.bt[:], ["bt"], ["Bb"])
+    quant("Tb", 0, 256, T.xt[:], ["xt"], ["Tbq", "Tbs"])
+
+    def first_max(lo, n, src, bank, cnt, tag):
+        op("v", lambda: V.tensor_tensor_scan(src[:, lo:lo + n], T["ps%d" % bank][:, 0:n], T.zer[:, 0:n], -1e29,
+                                             A.max, A.add), ["ps%d" % bank, "zer"], [tag])
+
+    def count(lo, n, src, cnt, tag, ctag):
+        op("a", lambda: S.activation(T.junk[:, 0:n], src[:, lo:lo + n], F.Sign, bias=src[:, lo + n - 1:lo + n],
+                                     scale=-1.0, accum_out=col(cnt)), [tag], [ctag, "junk"])
+
+    def latch(lo, bank, plo):
+        op("v", lambda: V.tensor_tensor_scan(T.D[:, lo:lo + 128], T.Am[:], T["ps%d" % bank][:, plo:plo + 128], 0.0,
+                                             A.add, A.max), ["ps%d" % bank, "Am"], ["D%d" % lo])
+
+    tb, bb, bo, bk = "Tb", "Bb", 0, ["Bb"]
+    for t in range(R_):
+        tk = [tb + "q", tb + "s"]
+        P, L, Aq, Bn, W, Tn = ["%s%d" % (n, t) for n in "PLABWT"]
+        offa, offb = "offa%d" % t, "offb%d" % t
+        owners = [[gr[2 * t + h] for gr in groups] for h in range(2)]
+        own = [h for h in range(2) if rank in owners[h]]
+
+        mm(0, 256, bb, bo, tb, 0, tk + bk)
+        mm(1, 128, tb, 0, bb, bo, tk + bk)
+        mm(2, 128, tb, 128, bb, bo, tk + bk)
+        first_max(0, 256, T.R, 0, JB, "R")
+        count(0, 256, T.R, JB, "R", "jb")
+        for h in range(2):
+            first_max(128 * h, 128, T.RT, 1 + h, KB + h, "RT%d" % h)
+        for h in range(2):
+            count(128 * h, 128, T.RT, KB + h, "RT%d" % h, "kb%d" % h)
+        for h in range(2):
+            ts(T.Ft[:, h:512:4], T.iJ[:, 128 * h:128 * h + 128], col(JB), None, A.is_equal, None,
+               ["iJ", "jb", "Fz"], ["Ft%d" % h])
+        quant("F", 0, 128, T.Ft[:], ["Ft0", "Ft1", "Fz"], ["F"])
+        mm(3, 256, "F", 0, "E", 0, ["F", "E0", "E1"])
+        for h in range(2):
+            ts(T.F2[:, 128 * h:128 * h + 128], T.iJ[:, 0:128], col(KB + h), 8.0, A.is_equal, A.mult,
+               ["iJ", "kb%d" % h], ["F2%d" % h])
+        for h in range(2):
+            op("v", lambda: V.tensor_tensor(T.Mt[:, h:512:4], T.ps3[:, 128 * h:128 * h + 128],
+                                            T.F2[:, 128 * h:128 * h + 128], A.mult),
+               ["ps3", "F2%d" % h, "Mz"], ["Mt%d" % h])
+        quant("M", 0, 128, T.Mt[:], ["Mt0", "Mt1", "Mz"], ["M"])
+        mm(0, 128, "C", 0, "M", 0, ["C", "M"])
+        mm(2, 128, "C", 256, "M", 0, ["C", "M"])
+        mm(1, 128, "C", 128, "M", 0, ["C", "M"])
+        mm(3, 128, "C", 384, "M", 0, ["C", "M"])
+        op("v", lambda: V.tensor_tensor_scan(T.qq[:], T.Ct[:, 0:512:4], T.ps0[:, 0:128], 0.0, A.add, A.subtract),
+           ["ps0", "C0"], ["qq"])
+        op("v", lambda: V.tensor_tensor(T.key[:], T.qq[:], T.ps1[:, 0:128], A.add), ["ps1", "qq"], ["key"])
+        for h in range(2):
+            op("a", lambda: S.activation(T.Ut[:, 2 + h:512:4], T["ps%d" % (2 + h)][:, 0:128], F.Copy,
+                                         accum_out=col(CC + h)), ["ps%d" % (2 + h)], ["Ut%d" % (2 + h), "cc%d" % h])
+        for h in range(2):
+            ts(T.Ut[:, h:512:4], T.key[:], col(CC + h), T.jc[:, h:h + 1], A.add, A.is_gt,
+               ["key", "cc%d" % h, "jc"], ["Ut%d" % h])
+        quant("U", 0, 128, T.Ut[:], ["Ut0", "Ut1", "Ut2", "Ut3"], ["U"])
+        mm(0, 128, "C", 0, "U", 0, ["C", "U"])
+        latch(0, 0, 0)
+        ts(T[offa][:], T.D[:, 15:128:16], col(CORR), None, A.subtract, None, ["D0", "corr"], [offa])
+        pick(P, 0, tb, 256, offa, 0, 8, [tb], P)
+
+        for kind, flip in (("q", 0), ("s", 1)):
+            parts = []
+            for h in range(2):
+                src = T[P + kind][:, H_ * h:H_ * h + H_]
+                dst = T[L + kind][:, H_ * rank:H_ * rank + H_]
+                if kind == "q":
+                    src, dst = src.bitcast(dt.uint8), dst.bitcast(dt.uint8)
+                parts.append((src, [(r, dst) for r in owners[h] if r != rank], halves[h ^ flip]))
+            send(parts, "p%d" % t, [P + kind])
+
+        op("a", lambda: S.activation(T.par[0:1, 128 * t:128 * t + 128], T.ps0[0:1, 0:128], F.Copy),
+           ["ps0"], ["par%d" % t])
+        dma("s", T.pa[t:t + 1, :], T.par[0:1, 128 * t:128 * t + 128], "out", ["par%d" % t], [])
+        if own:
+            h = own[0]
+            pick(L, H_ * rank, tb, 256, offa, 4 * h, 4 * h + 4, [tb], L + "o")
+            pick(L, H_ * NR, tb, 256, offa, 4 * h, 4 * h + 4, [tb], L + "p")
+            fill(T.At[:], 0.0, ["Az"])
+        if t == 0:
+            fill(T.Et[:, 1024:2048], 0.0, ["Ez2"])
+            make_e(2)
+            fill(T.Kt[:], 0.0, ["Kz"])
+            ts(T.j16[:], T.c16[:], col(PM), None, A.add, None, ["c16", "pm"], ["j16"])
+            quant(W, 0, 256, T.xt[:], ["xt"], [W + "aq", W + "as"])
+            quant("Ww", 0, 128, T.wt[:], ["wt"], ["Ww"])
+        else:
+            pw = "W%d" % (t - 1)
+            pick(W, 0, pw, 384, "offb%d" % (t - 1), 0, 16, [pw + "a", pw + "b"], W + "a")
+        for b in range(4):
+            mm(4 + b, 128, "E", 128 * b, P, 0, ["E%d" % b, P + "q", P + "s"], True, False)
+
+        if own:
+            h = own[0]
+            arrives("p%d" % t, (NR - 1) * 2 * len(halves[0]), [L])
+            lk = [L, L + "oq", L + "os", L + "pq", L + "ps"]
+            for b in (2, 3):
+                mm(b - 2, 512, "E", 128 * b, L, 0, lk + ["E%d" % b])
+            for r in range(NR):
+                for b in (0, 1):
+                    mm(2 + b, 128, "E", 128 * b, L, H_ * r, lk + ["E%d" % b], r == 0, r == NR - 1)
+            for r in range(NR):
+                for b in (2, 3):
+                    ac = T.acc[:, H_ * (b - 2):H_ * (b - 1)]
+                    src = T["ps%d" % (b - 2)][:, H_ * r:H_ * r + H_]
+                    if r == 0:
+                        op("v", lambda: V.tensor_copy(ac, src), ["ps%d" % (b - 2)], ["ac%d" % b])
+                    elif r < NR - 1:
+                        op("v", lambda: V.tensor_tensor(ac, ac, src, A.add), ["ps%d" % (b - 2), "ac%d" % b],
+                           ["ac%d" % b])
+                    else:
+                        op("v", lambda: V.tensor_tensor(T.At[:, 256 + b:512:4], ac, src, A.add),
+                           ["ps%d" % (b - 2), "ac%d" % b, "Az"], ["At%d" % b])
+            for b in (0, 1):
+                op("a", lambda: S.activation(T.At[:, 256 + b:512:4], T["ps%d" % (2 + b)][:, 0:H_], F.Copy),
+                   ["ps%d" % (2 + b), "Az"], ["At%d" % b])
+            ak = ["At0", "At1", "At2", "At3", "Az"]
+            quant(Aq, 0, 128, T.At[:, 256:768], ak, [Aq])
+            for kind in "qs":
+                src = T[Aq + kind][:, 0:H_]
+                dst = T[Bn + kind][:, H_ * (h + 1):H_ * (h + 2)]
+                if kind == "q":
+                    src, dst = src.bitcast(dt.uint8), dst.bitcast(dt.uint8)
+                send([(src, [(r, dst) for r in mine if r != rank], eng)], "b%d" % t, [Aq])
+            quant(Bn, 128 * h, 128 * h + 128, T.At[:, 256 * h:256 * h + 512], ak, [Bn + "o"])
+        arrives("b%d" % t, (2 - len(own)) * 2 * len(eng), [Bn])
+
+        for h in range(2):
+            op("v", lambda: V.tensor_reduce(col(MU + h), T.Mt[:, h:512:4], AxisListType.X, A.add),
+               ["Mt%d" % h], ["mu%d" % h])
+        for h in range(2):
+            ts(T.Ft[:, h:512:4], T.iJ[:, 0:128], col(KB + h), col(MU + h), A.is_le, A.mult,
+               ["iJ", "kb%d" % h, "mu%d" % h], ["Ft%d" % h])
+        quant("F", 0, 128, T.Ft[:], ["Ft0", "Ft1", "Fz"], ["F"])
+        mm(0, 256, "F", 0, "E", 0, ["F", "E0", "E1"])
+        ts(T.Kt[:, 0:1024:4], T.ps0[:, 0:256], 8.0, None, A.mult, None, ["ps0", "Kz"], ["Kt"])
+        quant("K", 0, 256, T.Kt[:], ["Kt", "Kz"], ["K"])
+        mm(1, 256, "C", 0, "K", 0, ["C", "K"])
+        latch(0, 1, 0)
+        latch(128, 1, 128)
+        ts(T.z16[:], T.D[:, 15:256:16], col(CORR), None, A.subtract, None, ["D0", "D128", "corr"], ["z16"])
+        ts(T.u16[:], T.z16[:], 0.0, C_ - 1.0, A.is_gt, A.mult, ["z16"], ["u16"])
+        op("v", lambda: V.tensor_tensor(T.v16[:], T.u16[:], T.z16[:], A.add), ["u16", "z16"], ["v16"])
+        op("v", lambda: V.tensor_tensor(T.w16[:], T.v16[:], T.j16[:], A.max), ["v16", "j16"], ["w16"])
+        op("v", lambda: V.tensor_copy(T[offb][:], T.w16[:]), ["w16"], [offb])
+
+        bb, bo, bk = Bn, H_, [Bn, Bn + "o"]
+        for b in range(4):
+            mm(4 + b, 128, "E", 128 * b, bb, bo, ["E%d" % b] + bk, False, True)
+        last = t == R_ - 1
+        if last:
+            mm(0, 128, "Ww", 0, bb, bo, ["Ww"] + bk)
+        for b in range(4):
+            src = T["ps%d" % (4 + b)][:, 0:128]
+            if b % 2 == 0:
+                ts(T.Vt[:, b:512:4], src, 4.0, None, A.mult, None, ["ps%d" % (4 + b)], ["Vt%d" % b])
+            else:
+                op("a", lambda: S.activation(T.Vt[:, b:512:4], src, F.Copy, scale=4.0),
+                   ["ps%d" % (4 + b)], ["Vt%d" % b])
+        if last:
+            op("a", lambda: S.activation(T.ysb[:, 256:384], T.ps0[:, 0:128], F.Copy), ["ps0"], ["yb"])
+            dma("s", T.y[:, 256:384], T.ysb[:, 256:384], "out", ["yb"], [])
+        quant(W, 256, 384, T.Vt[:], ["Vt0", "Vt1", "Vt2", "Vt3"], [W + "bq", W + "bs"])
+        pick(Tn, 0, W, 384, offb, 0, 16, [W + "a", W + "b"], Tn)
+        tb = Tn
+
+    tk = [tb + "q", tb + "s"]
+    dma("s", T.oc[:], T[tb + "q"][:].bitcast(dt.uint8), "out", [tb + "q"], [])
+    mm(1, 128, "Ww", 0, tb, 0, ["Ww"] + tk)
+    mm(2, 128, "Ww", 0, tb, 128, ["Ww"] + tk)
+    for k in range(4):
+        dma("s" if k < 2 else "a", T.osc[4 * k:4 * k + 4, :], T[tb + "s"][32 * k:32 * k + 4, :], "out",
+            [tb + "s"], [])
+    op("v", lambda: V.tensor_copy(T.ysb[:, 0:128], T.ps1[:, 0:128]), ["ps1"], ["y0"])
+    op("v", lambda: V.tensor_copy(T.ysb[:, 128:256], T.ps2[:, 0:128]), ["ps2"], ["y1"])
+    dma("s", T.y[:, 0:256], T.ysb[:, 0:256], "out", ["y0", "y1"], [])
+
+    for s in SEMAPHORES:
+        if total[s]:
+            g.wait_ge(T.sem[s], total[s])

@@ -19,9 +19,9 @@ def _mx(name, n):
 
 for _n, _w in (("xt", 1024), ("bt", 512), ("wt", 512), ("Et", 2048), ("Ct", 2048), ("Ft", 512), ("Mt", 512),
                ("Ut", 512), ("Kt", 1024), ("At", 768), ("Vt", 512), ("dI", 128), ("iJ", 256), ("i16", 128),
-               ("zer", 256), ("junk", 256), ("F2", 256), ("qq", 128), ("key", 128)):
+               ("zer", 128), ("junk", 256), ("F2", 256), ("qq", 128), ("key", 128)):
     _sb(_n, _w, "bfloat16")
-for _n, _w in (("R", 256), ("RT", 256), ("Am", 128), ("A0", 128), ("D", 256), ("cols", 16), ("jc", 2), ("acc", 128),
+for _n, _w in (("R", 256), ("RT", 256), ("Am", 128), ("A0", 128), ("D", 256), ("cols", 16), ("jc", 2), ("acc", 192),
                ("ysb", 384), ("par", 256), ("c16", 16), ("j16", 16), ("z16", 16), ("u16", 16), ("v16", 16),
                ("w16", 16)):
     _sb(_n, _w, "float32")
@@ -37,7 +37,7 @@ for _t in range(R_):
 for _i in range(8):
     SCRATCH["ps%d" % _i] = ("psum", [128, 512], "float32")
 
-SEMAPHORES = ["cv", "ca", "ct", "cg", "ldx", "ldb", "ldw", "out", "sent", "p0", "p1", "b0", "b1"]
+SEMAPHORES = ["cv", "ca", "ct", "cg", "ldx0", "ldx1", "ldb", "ldw", "out", "sent", "p0", "p1", "b0", "b1"]
 
 
 def _planes(T, topo):
@@ -145,6 +145,9 @@ def rank_program(g, core, T, topo):
     def fill(ap, val, wr):
         op("v", lambda: V.memset(ap, val), [], wr)
 
+    def afill(ap, n, val, wr):
+        op("a", lambda: S.activation(ap, T.Ct[:, 512:512 + n], F.Copy, scale=val / BIG), ["C1"], wr)
+
     def iota(ap, pattern, base, cm, wr, small=True):
         if small:
             op("g", lambda: g.iota(ap, pattern, base, cm, allow_small_or_imprecise_dtypes=True), [], wr)
@@ -173,14 +176,15 @@ def rank_program(g, core, T, topo):
     eng = [e for e in range(16) if all(e in topo.engines(core, c) for c in T.cores if c != core)]
     halves = [eng[:len(eng) // 2], eng[len(eng) // 2:]]
 
-    dma("s", T.xt[:], T.x[:], "ldx", [], ["xt"])
     dma("a", T.bt[:], T.b[:], "ldb", [], ["bt"])
-    dma("s", T.wt[:], T.w[:], "ldw", ["xt"], ["wt"])
+    dma("s", T.xt[:, 0:512], T.x[:, 0:512], "ldx0", [], ["xt0"])
+    dma("s", T.xt[:, 512:1024], T.x[:, 512:1024], "ldx1", [], ["xt1"])
+    dma("s", T.wt[:], T.w[:], "ldw", ["xt0", "xt1", "bt"], ["wt"])
 
     iota(T.dI[:], [[1, 128]], 0, -1, ["dI"])
-    iota(T.Ct[:, 0:512], [[0, 128], [-2, 2], [0, 2]], 1, 0, ["C0"])
-    iota(T.iJ[:], [[1, 256]], 0, 0, ["iJ"])
     iota(T.pint[:, 0:1], [[0, 1]], 0, 1, ["pi0"], small=False)
+    iota(T.zer[:], [[0, 128]], 0, 0, ["zer"])
+    iota(T.iJ[:], [[1, 256]], 0, 0, ["iJ"])
     iota(T.i16[:], [[0, 8], [1, 16]], 0, 0, ["i16"])
     iota(T.jc[:], [[128, 2]], 1, 1, ["jc"])
     iota(T.c16[:], [[16, 16]], 0, 0, ["c16"])
@@ -188,90 +192,107 @@ def rank_program(g, core, T, topo):
     def make_e(lo):
         for b in (lo, lo + 1):
             ts(T.Et[:, 512 * b + b:512 * (b + 1):4], T.dI[:], 0.0, 0.125, A.is_equal, A.mult,
-               ["dI", "Ez%d" % lo], ["Et%d" % b])
+               ["dI", "Ez%d" % b], ["Et%d" % b])
         quant("E", 128 * lo, 128 * lo + 256, T.Et[:, 512 * lo:512 * lo + 1024],
               ["Et%d" % lo, "Et%d" % (lo + 1)], ["E%d" % lo, "E%d" % (lo + 1)])
 
+    def cfill(tile, slots, val, key):
+        for i in slots:
+            afill(T.Ct[:, 512 * tile + i:512 * tile + 512:4], 128, val, ["%s%d" % (key, i)])
+
     fill(T.Ct[:, 512:1024], BIG, ["C1"])
-    fill(T.Et[:, 0:1024], 0.0, ["Ez0"])
-    fill(T.zer[:], 0.0, ["zer"])
-    fill(T.Ft[:], 0.0, ["Fz"])
-    fill(T.Mt[:], 0.0, ["Mz"])
-    op("a", lambda: S.activation(T.Ct[:, 1024:1536], T.Ct[:, 512:1024], F.Copy, scale=0.0), ["C1"], ["C2z"])
-    op("a", lambda: S.activation(T.Ct[:, 1536:2048], T.Ct[:, 512:1024], F.Copy, scale=1.0 / BIG), ["C1"], ["C3z"])
-    make_e(0)
-    ts(T.Ct[:, 1024:1536:4], T.dI[:], 0.0, None, A.is_ge, None, ["dI", "C2z"], ["C2"])
-    ts(T.Ct[:, 1537:2048:4], T.dI[:], 0.0, None, A.is_ge, None, ["dI", "C3z"], ["C3"])
-    quant("C", 0, 512, T.Ct[:], ["C0", "C1", "C2", "C3"], ["C"])
+    fill(T.Et[:, 0:1024], 0.0, ["Ez0", "Ez1"])
+    cfill(0, (0, 1), 1.0, "C0")
+    cfill(0, (2, 3), -1.0, "C0")
+    cfill(2, (1, 2, 3), 0.0, "C2")
+    cfill(3, (0, 2, 3), 1.0, "C3")
     ts(T.pint[:, 4:5], T.pint[:, 0:1], 15, None, A.bitwise_and, None, ["pi0"], ["pi1"])
+    ts(T.Ct[:, 1024:1536:4], T.dI[:], 0.0, None, A.is_ge, None, ["dI"], ["C20"])
     op("v", lambda: V.tensor_copy(col(PM), T.pint[:, 4:5]), ["pi1"], ["pm"])
-    ts(T.A0[:], T.i16[:], col(PM), DROP + STEP, A.not_equal, A.mult, ["i16", "pm"], ["A0"])
-    ts(col(CORR), col(PM), -STEP, 15 * STEP, A.mult, A.add, ["pm"], ["corr"])
-    op("a", lambda: S.activation(T.Am[:], T.A0[:], F.Identity, bias=-DROP), ["A0"], ["Am"])
+    ts(T.Ct[:, 1537:2048:4], T.dI[:], 0.0, None, A.is_ge, None, ["dI"], ["C31"])
+    make_e(0)
+    afill(T.Ft[:, 2:512:4], 128, 0.0, ["Fz2"])
+    afill(T.Ft[:, 3:512:4], 128, 0.0, ["Fz3"])
+    afill(T.Mt[:, 2:512:4], 128, 0.0, ["Mz2"])
+    afill(T.Mt[:, 3:512:4], 128, 0.0, ["Mz3"])
+    quant("C", 0, 512, T.Ct[:], ["C1"] + ["C%d%d" % (i, j) for i in (0, 2, 3) for j in range(4)], ["C"])
 
     quant("Bb", 0, 128, T.bt[:], ["bt"], ["Bb"])
-    quant("Tb", 0, 256, T.xt[:], ["xt"], ["Tbq", "Tbs"])
+    for h in range(2):
+        quant("Tb", 128 * h, 128 * h + 128, T.xt[:, 512 * h:512 * h + 512], ["xt%d" % h],
+              ["Tb%dq" % h, "Tb%ds" % h])
 
-    def first_max(lo, n, src, bank, cnt, tag):
-        op("v", lambda: V.tensor_tensor_scan(src[:, lo:lo + n], T["ps%d" % bank][:, 0:n], T.zer[:, 0:n], -1e29,
-                                             A.max, A.add), ["ps%d" % bank, "zer"], [tag])
+    def running_max(lo, dst, bank, init, rd, tag):
+        op("v", lambda: V.tensor_tensor_scan(dst[:, lo:lo + 128], T["ps%d" % bank][:, 0:128], T.zer[:], init,
+                                             A.max, A.add), ["ps%d" % bank, "zer"] + rd, [tag])
 
-    def count(lo, n, src, cnt, tag, ctag):
+    def count(lo, n, src, cnt, rd, ctag):
         op("a", lambda: S.activation(T.junk[:, 0:n], src[:, lo:lo + n], F.Sign, bias=src[:, lo + n - 1:lo + n],
-                                     scale=-1.0, accum_out=col(cnt)), [tag], [ctag, "junk"])
+                                     scale=-1.0, accum_out=col(cnt)), rd, [ctag, "junk"])
 
     def latch(lo, bank, plo):
         op("v", lambda: V.tensor_tensor_scan(T.D[:, lo:lo + 128], T.Am[:], T["ps%d" % bank][:, plo:plo + 128], 0.0,
                                              A.add, A.max), ["ps%d" % bank, "Am"], ["D%d" % lo])
 
+    LOW = -1e29
     tb, bb, bo, bk = "Tb", "Bb", 0, ["Bb"]
     for t in range(R_):
-        tk = [tb + "q", tb + "s"]
+        th = [[tb + "%dq" % h, tb + "%ds" % h] for h in range(2)]
+        tw = [tb + "0", tb + "1"]
         P, L, Aq, Bn, W, Tn = ["%s%d" % (n, t) for n in "PLABWT"]
         offa, offb = "offa%d" % t, "offb%d" % t
         owners = [[gr[2 * t + h] for gr in groups] for h in range(2)]
         own = [h for h in range(2) if rank in owners[h]]
 
-        mm(0, 256, bb, bo, tb, 0, tk + bk)
-        mm(1, 128, tb, 0, bb, bo, tk + bk)
-        mm(2, 128, tb, 128, bb, bo, tk + bk)
-        first_max(0, 256, T.R, 0, JB, "R")
-        count(0, 256, T.R, JB, "R", "jb")
+        mm(0, 128, bb, bo, tb, 0, th[0] + bk)
+        mm(4, 128, bb, bo, tb, 128, th[1] + bk)
+        mm(1, 128, tb, 0, bb, bo, th[0] + bk)
+        mm(2, 128, tb, 128, bb, bo, th[1] + bk)
+        running_max(0, T.R, 0, LOW, [], "R0")
+        running_max(128, T.R, 4, T.R[:, 127:128], ["R0"], "R1")
+        count(0, 256, T.R, JB, ["R0", "R1"], "jb")
         for h in range(2):
-            first_max(128 * h, 128, T.RT, 1 + h, KB + h, "RT%d" % h)
+            running_max(128 * h, T.RT, 1 + h, LOW, [], "RT%d" % h)
         for h in range(2):
-            count(128 * h, 128, T.RT, KB + h, "RT%d" % h, "kb%d" % h)
+            count(128 * h, 128, T.RT, KB + h, ["RT%d" % h], "kb%d" % h)
         for h in range(2):
             ts(T.Ft[:, h:512:4], T.iJ[:, 128 * h:128 * h + 128], col(JB), None, A.is_equal, None,
-               ["iJ", "jb", "Fz"], ["Ft%d" % h])
-        quant("F", 0, 128, T.Ft[:], ["Ft0", "Ft1", "Fz"], ["F"])
-        mm(3, 256, "F", 0, "E", 0, ["F", "E0", "E1"])
+               ["iJ", "jb"], ["Ft%d" % h])
+        quant("F", 0, 128, T.Ft[:], ["Ft0", "Ft1", "Fz2", "Fz3"], ["F"])
+        for h in range(2):
+            mm(3 + 2 * h, 128, "F", 0, "E", 128 * h, ["F", "E%d" % h])
         for h in range(2):
             ts(T.F2[:, 128 * h:128 * h + 128], T.iJ[:, 0:128], col(KB + h), 8.0, A.is_equal, A.mult,
                ["iJ", "kb%d" % h], ["F2%d" % h])
         for h in range(2):
-            op("v", lambda: V.tensor_tensor(T.Mt[:, h:512:4], T.ps3[:, 128 * h:128 * h + 128],
+            op("v", lambda: V.tensor_tensor(T.Mt[:, h:512:4], T["ps%d" % (3 + 2 * h)][:, 0:128],
                                             T.F2[:, 128 * h:128 * h + 128], A.mult),
-               ["ps3", "F2%d" % h, "Mz"], ["Mt%d" % h])
-        quant("M", 0, 128, T.Mt[:], ["Mt0", "Mt1", "Mz"], ["M"])
+               ["ps%d" % (3 + 2 * h), "F2%d" % h], ["Mt%d" % h])
+        quant("M", 0, 128, T.Mt[:], ["Mt0", "Mt1", "Mz2", "Mz3"], ["M"])
         mm(0, 128, "C", 0, "M", 0, ["C", "M"])
         mm(2, 128, "C", 256, "M", 0, ["C", "M"])
         mm(1, 128, "C", 128, "M", 0, ["C", "M"])
         mm(3, 128, "C", 384, "M", 0, ["C", "M"])
+        if t == 0:
+            ts(T.A0[:], T.i16[:], col(PM), DROP + STEP, A.not_equal, A.mult, ["i16", "pm"], ["A0"])
         op("v", lambda: V.tensor_tensor_scan(T.qq[:], T.Ct[:, 0:512:4], T.ps0[:, 0:128], 0.0, A.add, A.subtract),
-           ["ps0", "C0"], ["qq"])
+           ["ps0", "C00"], ["qq"])
         op("v", lambda: V.tensor_tensor(T.key[:], T.qq[:], T.ps1[:, 0:128], A.add), ["ps1", "qq"], ["key"])
         for h in range(2):
             op("a", lambda: S.activation(T.Ut[:, 2 + h:512:4], T["ps%d" % (2 + h)][:, 0:128], F.Copy,
                                          accum_out=col(CC + h)), ["ps%d" % (2 + h)], ["Ut%d" % (2 + h), "cc%d" % h])
+        if t == 0:
+            op("a", lambda: S.activation(T.Am[:], T.A0[:], F.Identity, bias=-DROP), ["A0"], ["Am"])
         for h in range(2):
             ts(T.Ut[:, h:512:4], T.key[:], col(CC + h), T.jc[:, h:h + 1], A.add, A.is_gt,
                ["key", "cc%d" % h, "jc"], ["Ut%d" % h])
         quant("U", 0, 128, T.Ut[:], ["Ut0", "Ut1", "Ut2", "Ut3"], ["U"])
         mm(0, 128, "C", 0, "U", 0, ["C", "U"])
+        if t == 0:
+            ts(col(CORR), col(PM), -STEP, 15 * STEP, A.mult, A.add, ["pm"], ["corr"])
         latch(0, 0, 0)
         ts(T[offa][:], T.D[:, 15:128:16], col(CORR), None, A.subtract, None, ["D0", "corr"], [offa])
-        pick(P, 0, tb, 256, offa, 0, 8, [tb], P)
+        pick(P, 0, tb, 256, offa, 0, 8, tw, P)
 
         for kind, flip in (("q", 0), ("s", 1)):
             parts = []
@@ -283,52 +304,59 @@ def rank_program(g, core, T, topo):
                 parts.append((src, [(r, dst) for r in owners[h] if r != rank], halves[h ^ flip]))
             send(parts, "p%d" % t, [P + kind])
 
-        op("a", lambda: S.activation(T.par[0:1, 128 * t:128 * t + 128], T.ps0[0:1, 0:128], F.Copy),
-           ["ps0"], ["par%d" % t])
-        dma("s", T.pa[t:t + 1, :], T.par[0:1, 128 * t:128 * t + 128], "out", ["par%d" % t], [])
+        if t == 0:
+            afill(T.Et[:, 1024:1536], 512, 0.0, ["Ez2"])
+            fill(T.Et[:, 1536:2048], 0.0, ["Ez3"])
         if own:
             h = own[0]
-            pick(L, H_ * rank, tb, 256, offa, 4 * h, 4 * h + 4, [tb], L + "o")
-            pick(L, H_ * NR, tb, 256, offa, 4 * h, 4 * h + 4, [tb], L + "p")
-            fill(T.At[:], 0.0, ["Az"])
+            pick(L, H_ * rank, tb, 256, offa, 4 * h, 4 * h + 4, tw, L + "o")
+            pick(L, H_ * NR, tb, 256, offa, 4 * h, 4 * h + 4, tw, L + "p")
+        op("a", lambda: S.activation(T.par[0:1, 128 * t:128 * t + 128], T.ps0[0:1, 0:128], F.Copy),
+           ["ps0"], ["par%d" % t])
         if t == 0:
-            fill(T.Et[:, 1024:2048], 0.0, ["Ez2"])
             make_e(2)
-            fill(T.Kt[:], 0.0, ["Kz"])
-            ts(T.j16[:], T.c16[:], col(PM), None, A.add, None, ["c16", "pm"], ["j16"])
-            quant(W, 0, 256, T.xt[:], ["xt"], [W + "aq", W + "as"])
-            quant("Ww", 0, 128, T.wt[:], ["wt"], ["Ww"])
-        else:
-            pw = "W%d" % (t - 1)
-            pick(W, 0, pw, 384, "offb%d" % (t - 1), 0, 16, [pw + "a", pw + "b"], W + "a")
-        for b in range(4):
-            mm(4 + b, 128, "E", 128 * b, P, 0, ["E%d" % b, P + "q", P + "s"], True, False)
+            afill(T.Kt[:, 0:512], 512, 0.0, ["Kz0"])
+            afill(T.Kt[:, 512:1024], 512, 0.0, ["Kz1"])
+        if own:
+            afill(T.At[:, 0:256], 256, 0.0, ["Az0"])
+            afill(T.At[:, 512:768], 256, 0.0, ["Az1"])
+        dma("s", T.pa[t:t + 1, :], T.par[0:1, 128 * t:128 * t + 128], "out", ["par%d" % t], [])
+        for h in range(2):
+            op("v", lambda: V.tensor_reduce(col(MU + h), T.Mt[:, h:512:4], AxisListType.X, A.add),
+               ["Mt%d" % h], ["mu%d" % h])
+        for h in range(2):
+            ts(T.Ft[:, h:512:4], T.iJ[:, 0:128], col(KB + h), col(MU + h), A.is_le, A.mult,
+               ["iJ", "kb%d" % h, "mu%d" % h], ["Ft%d" % h])
+        quant("F", 0, 128, T.Ft[:], ["Ft0", "Ft1", "Fz2", "Fz3"], ["F"])
+        mm(2, 256, "F", 0, "E", 0, ["F", "E0", "E1"])
+        ts(T.Kt[:, 0:1024:4], T.ps2[:, 0:256], 8.0, None, A.mult, None, ["ps2", "Kz0", "Kz1"], ["Kt"])
+        quant("K", 0, 256, T.Kt[:], ["Kt", "Kz0", "Kz1"], ["K"])
 
         if own:
             h = own[0]
             arrives("p%d" % t, (NR - 1) * 2 * len(halves[0]), [L])
             lk = [L, L + "oq", L + "os", L + "pq", L + "ps"]
-            for b in (2, 3):
-                mm(b - 2, 512, "E", 128 * b, L, 0, lk + ["E%d" % b])
+            for part in range(2):
+                for b in (1, 2, 3):
+                    mm(b - 1 + 4 * part, 256, "E", 128 * b, L, 256 * part, lk + ["E%d" % b])
             for r in range(NR):
-                for b in (0, 1):
-                    mm(2 + b, 128, "E", 128 * b, L, H_ * r, lk + ["E%d" % b], r == 0, r == NR - 1)
-            for r in range(NR):
-                for b in (2, 3):
-                    ac = T.acc[:, H_ * (b - 2):H_ * (b - 1)]
-                    src = T["ps%d" % (b - 2)][:, H_ * r:H_ * r + H_]
-                    if r == 0:
-                        op("v", lambda: V.tensor_copy(ac, src), ["ps%d" % (b - 2)], ["ac%d" % b])
-                    elif r < NR - 1:
-                        op("v", lambda: V.tensor_tensor(ac, ac, src, A.add), ["ps%d" % (b - 2), "ac%d" % b],
-                           ["ac%d" % b])
-                    else:
-                        op("v", lambda: V.tensor_tensor(T.At[:, 256 + b:512:4], ac, src, A.add),
-                           ["ps%d" % (b - 2), "ac%d" % b, "Az"], ["At%d" % b])
-            for b in (0, 1):
-                op("a", lambda: S.activation(T.At[:, 256 + b:512:4], T["ps%d" % (2 + b)][:, 0:H_], F.Copy),
-                   ["ps%d" % (2 + b), "Az"], ["At%d" % b])
-            ak = ["At0", "At1", "At2", "At3", "Az"]
+                mm(3, 128, "E", 0, L, H_ * r, lk + ["E0"], r == 0, r == NR - 1)
+            steps = sorted((r + (b - 1), -b, r, b) for r in range(NR) for b in (1, 2, 3))
+            for _, _, r, b in steps:
+                ac = T.acc[:, H_ * (b - 1):H_ * b]
+                bank = "ps%d" % (b - 1 + 4 * (r // 4))
+                src = T[bank][:, H_ * (r % 4):H_ * (r % 4) + H_]
+                if r == 0 and b < 3:
+                    op("v", lambda: V.tensor_copy(ac, src), [bank], ["ac%d" % b])
+                elif r == 0:
+                    op("a", lambda: S.activation(ac, src, F.Copy), [bank], ["ac%d" % b])
+                elif r < NR - 1:
+                    op("v", lambda: V.tensor_tensor(ac, ac, src, A.add), [bank, "ac%d" % b], ["ac%d" % b])
+                else:
+                    op("v", lambda: V.tensor_tensor(T.At[:, 256 + b:512:4], ac, src, A.add),
+                       [bank, "ac%d" % b], ["At%d" % b])
+            op("a", lambda: S.activation(T.At[:, 256:512:4], T.ps3[:, 0:H_], F.Copy), ["ps3"], ["At0"])
+            ak = ["At0", "At1", "At2", "At3", "Az0", "Az1"]
             quant(Aq, 0, 128, T.At[:, 256:768], ak, [Aq])
             for kind in "qs":
                 src = T[Aq + kind][:, 0:H_]
@@ -336,24 +364,26 @@ def rank_program(g, core, T, topo):
                 if kind == "q":
                     src, dst = src.bitcast(dt.uint8), dst.bitcast(dt.uint8)
                 send([(src, [(r, dst) for r in mine if r != rank], eng)], "b%d" % t, [Aq])
-            quant(Bn, 128 * h, 128 * h + 128, T.At[:, 256 * h:256 * h + 512], ak, [Bn + "o"])
         arrives("b%d" % t, (2 - len(own)) * 2 * len(eng), [Bn])
 
-        for h in range(2):
-            op("v", lambda: V.tensor_reduce(col(MU + h), T.Mt[:, h:512:4], AxisListType.X, A.add),
-               ["Mt%d" % h], ["mu%d" % h])
-        for h in range(2):
-            ts(T.Ft[:, h:512:4], T.iJ[:, 0:128], col(KB + h), col(MU + h), A.is_le, A.mult,
-               ["iJ", "kb%d" % h, "mu%d" % h], ["Ft%d" % h])
-        quant("F", 0, 128, T.Ft[:], ["Ft0", "Ft1", "Fz"], ["F"])
-        mm(0, 256, "F", 0, "E", 0, ["F", "E0", "E1"])
-        ts(T.Kt[:, 0:1024:4], T.ps0[:, 0:256], 8.0, None, A.mult, None, ["ps0", "Kz"], ["Kt"])
-        quant("K", 0, 256, T.Kt[:], ["Kt", "Kz"], ["K"])
         mm(1, 256, "C", 0, "K", 0, ["C", "K"])
+        for b in range(4):
+            mm(4 + b, 128, "E", 128 * b, P, 0, ["E%d" % b, P + "q", P + "s"], True, False)
+        if own:
+            quant(Bn, 128 * h, 128 * h + 128, T.At[:, 256 * h:256 * h + 512], ak, [Bn + "o"])
         latch(0, 1, 0)
         latch(128, 1, 128)
+        if t == 0:
+            ts(T.j16[:], T.c16[:], col(PM), None, A.add, None, ["c16", "pm"], ["j16"])
         ts(T.z16[:], T.D[:, 15:256:16], col(CORR), None, A.subtract, None, ["D0", "D128", "corr"], ["z16"])
+        if t == 0:
+            quant(W, 0, 256, T.xt[:], ["xt0", "xt1"], [W + "aq", W + "as"])
+        else:
+            pw = "W%d" % (t - 1)
+            pick(W, 0, pw, 384, "offb%d" % (t - 1), 0, 16, [pw + "a", pw + "b"], W + "a")
         ts(T.u16[:], T.z16[:], 0.0, C_ - 1.0, A.is_gt, A.mult, ["z16"], ["u16"])
+        if t == 0:
+            quant("Ww", 0, 128, T.wt[:], ["wt"], ["Ww"])
         op("v", lambda: V.tensor_tensor(T.v16[:], T.u16[:], T.z16[:], A.add), ["u16", "z16"], ["v16"])
         op("v", lambda: V.tensor_tensor(T.w16[:], T.v16[:], T.j16[:], A.max), ["v16", "j16"], ["w16"])
         op("v", lambda: V.tensor_copy(T[offb][:], T.w16[:]), ["w16"], [offb])
@@ -366,7 +396,7 @@ def rank_program(g, core, T, topo):
             mm(0, 128, "Ww", 0, bb, bo, ["Ww"] + bk)
         for b in range(4):
             src = T["ps%d" % (4 + b)][:, 0:128]
-            if b % 2 == 0:
+            if b % 2 == 1:
                 ts(T.Vt[:, b:512:4], src, 4.0, None, A.mult, None, ["ps%d" % (4 + b)], ["Vt%d" % b])
             else:
                 op("a", lambda: S.activation(T.Vt[:, b:512:4], src, F.Copy, scale=4.0),
@@ -375,19 +405,23 @@ def rank_program(g, core, T, topo):
             op("a", lambda: S.activation(T.ysb[:, 256:384], T.ps0[:, 0:128], F.Copy), ["ps0"], ["yb"])
             dma("s", T.y[:, 256:384], T.ysb[:, 256:384], "out", ["yb"], [])
         quant(W, 256, 384, T.Vt[:], ["Vt0", "Vt1", "Vt2", "Vt3"], [W + "bq", W + "bs"])
-        pick(Tn, 0, W, 384, offb, 0, 16, [W + "a", W + "b"], Tn)
+        for h in range(2):
+            pick(Tn, 128 * h, W, 384, offb, 8 * h, 8 * h + 8, [W + "a", W + "b"], Tn + "%d" % h)
         tb = Tn
 
-    tk = [tb + "q", tb + "s"]
-    dma("s", T.oc[:], T[tb + "q"][:].bitcast(dt.uint8), "out", [tb + "q"], [])
-    mm(1, 128, "Ww", 0, tb, 0, ["Ww"] + tk)
-    mm(2, 128, "Ww", 0, tb, 128, ["Ww"] + tk)
-    for k in range(4):
-        dma("s" if k < 2 else "a", T.osc[4 * k:4 * k + 4, :], T[tb + "s"][32 * k:32 * k + 4, :], "out",
-            [tb + "s"], [])
-    op("v", lambda: V.tensor_copy(T.ysb[:, 0:128], T.ps1[:, 0:128]), ["ps1"], ["y0"])
-    op("v", lambda: V.tensor_copy(T.ysb[:, 128:256], T.ps2[:, 0:128]), ["ps2"], ["y1"])
-    dma("s", T.y[:, 0:256], T.ysb[:, 0:256], "out", ["y0", "y1"], [])
+    def scales_out(q, k):
+        dma(q, T.osc[4 * k:4 * k + 4, :], T[tb + "s"][32 * k:32 * k + 4, :], "out", [tb + "0s", tb + "1s"], [])
+    for h in range(2):
+        mm(1 + h, 128, "Ww", 0, tb, 128 * h, ["Ww", tb + "%dq" % h, tb + "%ds" % h])
+        dma("s", T.oc[:, 512 * h:512 * h + 512], T[tb + "q"][:, 128 * h:128 * h + 128].bitcast(dt.uint8), "out",
+            [tb + "%dq" % h], [])
+    scales_out("a", 3)
+    for k in range(3):
+        scales_out("s", k)
+    for h in range(2):
+        op("v", lambda: V.tensor_copy(T.ysb[:, 128 * h:128 * h + 128], T["ps%d" % (1 + h)][:, 0:128]),
+           ["ps%d" % (1 + h)], ["y%d" % h])
+        dma("a", T.y[:, 128 * h:128 * h + 128], T.ysb[:, 128 * h:128 * h + 128], "out", ["y%d" % h], [])
 
     for s in SEMAPHORES:
         if total[s]:

@@ -1,9 +1,10 @@
 from concourse.bass import DstId, RemoteDMATransfer
 from concourse.mybir import dt, AluOpType, AxisListType, ActivationFunctionType
 
-R_, C_, K_, H_ = 2, 256, 128, 64
+R_, C_, K_ = 2, 256, 128
 NR = 8
-STEP, DROP, BIG = 512.0, 16384.0, 512.0
+Q_ = 32
+STEP, DROP = 512.0, 16384.0
 
 SCRATCH = {}
 
@@ -17,27 +18,31 @@ def _mx(name, n):
     _sb(name + "s", n, "uint8")
 
 
-for _n, _w in (("xt", 1024), ("bt", 512), ("wt", 512), ("Et", 2048), ("Ct", 2048), ("Ft", 512), ("Mt", 512),
-               ("Ut", 512), ("Kt", 1024), ("At", 768), ("Vt", 512), ("dI", 128), ("iJ", 256), ("i16", 128),
-               ("zer", 128), ("junk", 256), ("F2", 256), ("qq", 128), ("key", 128)):
+for _n, _w in (("xt", 1024), ("bt", 512), ("wt", 512), ("Et", 520), ("Jt", 520), ("Ct", 1536), ("Ft", 512),
+               ("Mt", 520), ("Ut", 520), ("Kt", 1024), ("At", 512), ("Vt", 512), ("dI", 128), ("iP", 256),
+               ("i16", 128), ("zer", 256), ("junk", 256), ("key", 128), ("msk", NR * Q_), ("Z", 3 * NR * Q_)):
     _sb(_n, _w, "bfloat16")
-for _n, _w in (("R", 256), ("RT", 256), ("Am", 128), ("A0", 128), ("D", 256), ("cols", 16), ("jc", 2), ("acc", 192),
+for _n, _w in (("R", 256), ("RT", 256), ("qq", 128), ("Am", 128), ("A0", 128), ("D", 256), ("cols", 16),
                ("ysb", 384), ("par", 256), ("c16", 16), ("j16", 16), ("z16", 16), ("u16", 16), ("v16", 16),
                ("w16", 16)):
     _sb(_n, _w, "float32")
 _sb("pint", 8, "int32")
-for _n, _w in (("E", 512), ("C", 512), ("Bb", 128), ("Tb", 256), ("Ww", 128), ("F", 128), ("M", 128), ("U", 128),
-               ("K", 256)):
+_sb("offi", 16, "uint16")
+_sb("offo", 16, "uint16")
+for _n, _w in (("E", 512), ("J", 256), ("C", 384), ("Bb", 128), ("W%d" % R_, 256), ("Ww", 128), ("F", 128),
+               ("M", 130), ("U", 128), ("K", 256)):
     _mx(_n, _w)
 for _t in range(R_):
     _sb("offa%d" % _t, 8, "uint16")
     _sb("offb%d" % _t, 16, "uint16")
-    for _n, _w in (("P", 128), ("L", 576), ("A", 128), ("B", 256), ("W", 384), ("T", 256)):
+    for _n, _w in (("P", 128), ("L", (NR - 1) * Q_ + 128), ("I", NR * Q_), ("A", 128), ("B", 128), ("W", 384)):
         _mx("%s%d" % (_n, _t), _w)
+    _sb("H%d" % _t, K_, "uint8")
 for _i in range(8):
     SCRATCH["ps%d" % _i] = ("psum", [128, 512], "float32")
 
-SEMAPHORES = ["cv", "ca", "ct", "cg", "ldx0", "ldx1", "ldb", "ldw", "out", "sent", "p0", "p1", "b0", "b1"]
+SEMAPHORES = ["cv", "ca", "ct", "cg", "ldx0", "ldx1", "ldb", "ldw", "out", "sent", "p0", "p1", "b0", "b1",
+              "h0", "h1", "s0", "s1"]
 
 
 def _planes(T, topo):
@@ -52,9 +57,68 @@ def _planes(T, topo):
     return groups
 
 
+def _helpers(T, topo, rank):
+    core = T.cores[rank]
+    near = sorted((c for c in topo.cores_of(core) if c not in T.cores), key=lambda c: topo.die(c) != topo.die(core))
+    found = []
+    for gr in sorted(_planes(T, topo), key=lambda gr: rank in gr):
+        c = [c for c in near if c not in [f for f, _ in found] and all(topo.may_write(c, T.cores[r]) for r in gr)][0]
+        found.append((c, gr))
+    return found
+
+
+def _write(T, topo, src, dsts, eng, sem):
+    ids = []
+    for c, _ in dsts:
+        rid, pid, _e = topo.addr(c)
+        ids.append(DstId(rid=rid, pnc=pid))
+    return RemoteDMATransfer(dst_ids=ids, dma_engine_mask=sum(1 << e for e in eng), remote_sem=T.sem[sem], src=src,
+                             dsts=[d for _, d in dsts])
+
+
+def _engines(T, topo, core):
+    beside = topo.engines(core, [c for c in topo.cores_of(core) if c != core][0])
+    off = [c for c in T.cores if topo.chip(c) != topo.chip(core)]
+    far = [e for e in beside if all(e in topo.engines(core, c) for c in off)]
+    return far, [e for e in beside if e not in far]
+
+
+def _code_calls(T, topo, rank):
+    groups = _planes(T, topo)
+    mine = [gr for gr in groups if rank in gr][0]
+    other = [gr for gr in groups if gr is not mine][0]
+    me, nq = mine.index(rank), len(mine)
+    far = _engines(T, topo, T.cores[rank])[0]
+    turn = [(me + i) % nq for i in range(1, nq)]
+    calls = [[(u, mine[u]) for u in turn] + [(me, other[me])], [(u, other[u]) for u in turn[:2]],
+             [(turn[2], other[turn[2]])]]
+    return [[(u, r, far[i * len(far) // len(call):(i + 1) * len(far) // len(call)]) for i, (u, r) in enumerate(call)]
+            for call in calls]
+
+
+def _hand_on(g, core, T, topo):
+    for rank in range(NR):
+        for c, gr in _helpers(T, topo, rank):
+            if c != core:
+                continue
+            far = _engines(T, topo, core)[0]
+            home = _engines(T, topo, T.cores[rank])[1]
+            ne = len(far) // len(gr)
+            sent = 0
+            for t in range(R_):
+                g.wait_ge(T.sem["h%d" % t], len(home))
+                trs = [_write(T, topo, T["H%d" % t][:, Q_ * u:Q_ * u + Q_],
+                              [(T.cores[r], T["L%ds" % t][:, Q_ * rank:Q_ * rank + Q_])], far[ne * u:ne * u + ne],
+                              "s%d" % t) for u, r in enumerate(gr) if r != rank]
+                g.remote_dma_fused(trs, local_sem=T.sem.sent)
+                sent += ne * len(trs)
+            g.wait_ge(T.sem.sent, sent)
+
+
 def rank_program(g, core, T, topo):
     rank = T.rank_of(core)
     if rank is None:
+        _hand_on(g, core, T, topo)
         return
     A = AluOpType
     F = ActivationFunctionType
@@ -127,14 +191,20 @@ def rank_program(g, core, T, topo):
                                      T[x + "q"][:, xa:xa + n], T[x + "s"][:, xa:xa + n], start, stop),
            rd, ["ps%d" % bank])
 
-    def pick(dst, da, src, sn, off, oa, ob, rd, key):
+    def pick_codes(dst, da, src, sn, off, oa, ob, rd, key):
         n = 16 * (ob - oa)
         op("v", lambda: V.tensor_copy(T[dst + "q"][:, da:da + n].bitcast(dt.uint32),
                                       T[src + "q"][:, 0:sn].bitcast(dt.uint32).indirect(T[off][:, oa:ob])),
            [k + "q" for k in rd] + [off], [key + "q"])
-        op("a", lambda: S.activation(T[dst + "s"][:, da:da + n], T[src + "s"][:, 0:sn].indirect(T[off][:, oa:ob]),
-                                     F.Copy),
+
+    def pick_scales(q, dst, da, src, sn, off, oa, ob, rd, key):
+        out, win = T[dst + "s"][:, da:da + 16 * (ob - oa)], T[src + "s"][:, 0:sn].indirect(T[off][:, oa:ob])
+        op(q, (lambda: S.activation(out, win, F.Copy)) if q == "a" else (lambda: V.tensor_copy(out, win)),
            [k + "s" for k in rd] + [off], [key + "s"])
+
+    def pick(*args):
+        pick_codes(*args)
+        pick_scales("a", *args)
 
     def ts(out, in0, s1, s2, op0, op1, rd, wr):
         if op1 is None:
@@ -146,7 +216,7 @@ def rank_program(g, core, T, topo):
         op("v", lambda: V.memset(ap, val), [], wr)
 
     def afill(ap, n, val, wr):
-        op("a", lambda: S.activation(ap, T.Ct[:, 512:512 + n], F.Copy, scale=val / BIG), ["C1"], wr)
+        op("a", lambda: S.activation(ap, T.zer[:, 0:n], F.Identity, bias=val), ["zer"], wr)
 
     def iota(ap, pattern, base, cm, wr, small=True):
         if small:
@@ -156,25 +226,20 @@ def rank_program(g, core, T, topo):
 
     def send(parts, sem, rd):
         deps("g", rd, [])
-        trs = []
-        for src, dsts, eng in parts:
-            ids = []
-            for r, _ in dsts:
-                rid, pid, _e = topo.addr(T.cores[r])
-                ids.append(DstId(rid=rid, pnc=pid))
-            trs.append(RemoteDMATransfer(dst_ids=ids, dma_engine_mask=sum(1 << e for e in eng),
-                                         remote_sem=T.sem[sem], src=src, dsts=[d for _, d in dsts]))
-            total["sent"] += len(eng)
-        g.remote_dma_fused(trs, local_sem=T.sem.sent)
+        g.remote_dma_fused([_write(T, topo, src, dsts, es, sem) for src, dsts, es in parts], local_sem=T.sem.sent)
+        total["sent"] += sum(len(es) for _, _, es in parts)
 
     def col(i):
         return T.cols[:, i:i + 1]
-    JB, KB, CC, MU, PM, CORR = 0, 1, 3, 5, 7, 8
+    JB, KB, CC, MU, PM, CORR, G8, IL = 0, 1, 3, 5, 7, 8, 9, 10
 
-    groups = _planes(T, topo)
-    mine = [gr for gr in groups if rank in gr][0]
-    eng = [e for e in range(16) if all(e in topo.engines(core, c) for c in T.cores if c != core)]
-    halves = [eng[:len(eng) // 2], eng[len(eng) // 2:]]
+    mine = [gr for gr in _planes(T, topo) if rank in gr][0]
+    me = mine.index(rank)
+    nq = len(mine)
+    peers = [mine[(me + i) % nq] for i in range(1, nq)]
+    eng, home = _engines(T, topo, core)
+    ne = len(eng) // nq
+    landed = sum(len(es) for s in range(NR) for call in _code_calls(T, topo, s) for _, r, es in call if r == rank)
 
     dma("a", T.bt[:], T.b[:], "ldb", [], ["bt"])
     dma("s", T.xt[:, 0:512], T.x[:, 0:512], "ldx0", [], ["xt0"])
@@ -183,47 +248,38 @@ def rank_program(g, core, T, topo):
 
     iota(T.dI[:], [[1, 128]], 0, -1, ["dI"])
     iota(T.pint[:, 0:1], [[0, 1]], 0, 1, ["pi0"], small=False)
-    iota(T.zer[:], [[0, 128]], 0, 0, ["zer"])
-    iota(T.iJ[:], [[1, 256]], 0, 0, ["iJ"])
+    iota(T.iP[:], [[1, 128], [128, 2]], 0, 0, ["iP"])
     iota(T.i16[:], [[0, 8], [1, 16]], 0, 0, ["i16"])
-    iota(T.jc[:], [[128, 2]], 1, 1, ["jc"])
     iota(T.c16[:], [[16, 16]], 0, 0, ["c16"])
 
-    def make_e(lo):
-        for b in (lo, lo + 1):
-            ts(T.Et[:, 512 * b + b:512 * (b + 1):4], T.dI[:], 0.0, 0.125, A.is_equal, A.mult,
-               ["dI", "Ez%d" % b], ["Et%d" % b])
-        quant("E", 128 * lo, 128 * lo + 256, T.Et[:, 512 * lo:512 * lo + 1024],
-              ["Et%d" % lo, "Et%d" % (lo + 1)], ["E%d" % lo, "E%d" % (lo + 1)])
-
-    def cfill(tile, slots, val, key):
-        for i in slots:
-            afill(T.Ct[:, 512 * tile + i:512 * tile + 512:4], 128, val, ["%s%d" % (key, i)])
-
-    fill(T.Ct[:, 512:1024], BIG, ["C1"])
-    fill(T.Et[:, 0:1024], 0.0, ["Ez0", "Ez1"])
-    cfill(0, (0, 1), 1.0, "C0")
-    cfill(0, (2, 3), -1.0, "C0")
-    cfill(2, (1, 2, 3), 0.0, "C2")
-    cfill(3, (0, 2, 3), 1.0, "C3")
-    ts(T.pint[:, 4:5], T.pint[:, 0:1], 15, None, A.bitwise_and, None, ["pi0"], ["pi1"])
-    ts(T.Ct[:, 1024:1536:4], T.dI[:], 0.0, None, A.is_ge, None, ["dI"], ["C20"])
-    op("v", lambda: V.tensor_copy(col(PM), T.pint[:, 4:5]), ["pi1"], ["pm"])
-    ts(T.Ct[:, 1537:2048:4], T.dI[:], 0.0, None, A.is_ge, None, ["dI"], ["C31"])
-    make_e(0)
-    afill(T.Ft[:, 2:512:4], 128, 0.0, ["Fz2"])
-    afill(T.Ft[:, 3:512:4], 128, 0.0, ["Fz3"])
-    afill(T.Mt[:, 2:512:4], 128, 0.0, ["Mz2"])
-    afill(T.Mt[:, 3:512:4], 128, 0.0, ["Mz3"])
-    quant("C", 0, 512, T.Ct[:], ["C1"] + ["C%d%d" % (i, j) for i in (0, 2, 3) for j in range(4)], ["C"])
+    fill(T.zer[:], 0.0, ["zer"])
+    fill(T.Jt[:], 0.0, ["Jz"])
+    fill(T.Ct[:, 3:1536:4], 1.0, ["Ca"])
+    afill(T.Ct[:, 0:512:2], 256, -1.0, ["Cb"])
+    afill(T.Ct[:, 513:1536:4], 256, 0.0, ["Cd"])
+    afill(T.Ct[:, 1:512:4], 128, 1.0, ["Cc"])
+    afill(T.Ct[:, 514:1024:4], 128, 1.0, ["Ce"])
+    afill(T.Ct[:, 1024:1536:4], 128, 0.0, ["Cf"])
+    afill(T.Ft[:, 1:512:2], 256, 1.0, ["Fz"])
+    afill(T.Mt[:, 1:512:4], 128, 1.0 / 128, ["Ma"])
+    afill(T.Mt[:, 3:512:4], 128, 0.0, ["Mb"])
+    afill(T.Mt[:, 512:520:2], 4, -0.5, ["Mc"])
+    afill(T.Mt[:, 513:520:2], 4, 0.5, ["Md"])
+    ts(T.Jt[:, 2:514:4], T.dI[:], 0.0, 128.0, A.is_equal, A.mult, ["dI", "Jz"], ["Ja"])
+    ts(T.Jt[:, 3:514:4], T.dI[:], 0.0, None, A.is_gt, None, ["dI", "Jz"], ["Jb"])
+    ts(T.Ct[:, 512:1024:4], T.dI[:], 0.0, None, A.is_lt, None, ["dI"], ["Cg"])
+    ts(T.Ct[:, 1026:1536:4], T.dI[:], 0.0, None, A.is_lt, None, ["dI"], ["Ch"])
+    for h in range(2):
+        quant("J", 128 * h, 128 * h + 128, T.Jt[:, 2 - 2 * h:514 - 2 * h], ["Ja", "Jb"], ["J%d" % h])
+    quant("C", 0, 384, T.Ct[:], ["C" + c for c in "abcdefgh"], ["C"])
 
     quant("Bb", 0, 128, T.bt[:], ["bt"], ["Bb"])
     for h in range(2):
-        quant("Tb", 128 * h, 128 * h + 128, T.xt[:, 512 * h:512 * h + 512], ["xt%d" % h],
-              ["Tb%dq" % h, "Tb%ds" % h])
+        quant("W0", 128 * h, 128 * h + 128, T.xt[:, 512 * h:512 * h + 512], ["xt%d" % h],
+              ["W0%dq" % h, "W0%ds" % h])
 
     def running_max(lo, dst, bank, init, rd, tag):
-        op("v", lambda: V.tensor_tensor_scan(dst[:, lo:lo + 128], T["ps%d" % bank][:, 0:128], T.zer[:], init,
+        op("v", lambda: V.tensor_tensor_scan(dst[:, lo:lo + 128], T["ps%d" % bank][:, 0:128], T.zer[:, 0:128], init,
                                              A.max, A.add), ["ps%d" % bank, "zer"] + rd, [tag])
 
     def count(lo, n, src, cnt, rd, ctag):
@@ -235,19 +291,19 @@ def rank_program(g, core, T, topo):
                                              A.add, A.max), ["ps%d" % bank, "Am"], ["D%d" % lo])
 
     LOW = -1e29
-    tb, bb, bo, bk = "Tb", "Bb", 0, ["Bb"]
+    NI = NR * Q_
+    bb, bk = "Bb", ["Bb"]
     for t in range(R_):
-        th = [[tb + "%dq" % h, tb + "%ds" % h] for h in range(2)]
-        tw = [tb + "0", tb + "1"]
-        P, L, Aq, Bn, W, Tn = ["%s%d" % (n, t) for n in "PLABWT"]
+        P, L, I, Aq, Bn, W = ["%s%d" % (n, t) for n in "PLIABW"]
+        Wn = "W%d" % (t + 1)
+        th = [[W + "%dq" % h, W + "%ds" % h] for h in range(2)]
+        tw = [W + "0", W + "1"]
         offa, offb = "offa%d" % t, "offb%d" % t
-        owners = [[gr[2 * t + h] for gr in groups] for h in range(2)]
-        own = [h for h in range(2) if rank in owners[h]]
 
-        mm(0, 128, bb, bo, tb, 0, th[0] + bk)
-        mm(4, 128, bb, bo, tb, 128, th[1] + bk)
-        mm(1, 128, tb, 0, bb, bo, th[0] + bk)
-        mm(2, 128, tb, 128, bb, bo, th[1] + bk)
+        mm(0, 128, bb, 0, W, 0, th[0] + bk)
+        mm(4, 128, bb, 0, W, 128, th[1] + bk)
+        mm(1, 128, W, 0, bb, 0, th[0] + bk)
+        mm(2, 128, W, 128, bb, 0, th[1] + bk)
         running_max(0, T.R, 0, LOW, [], "R0")
         running_max(128, T.R, 4, T.R[:, 127:128], ["R0"], "R1")
         count(0, 256, T.R, JB, ["R0", "R1"], "jb")
@@ -255,145 +311,140 @@ def rank_program(g, core, T, topo):
             running_max(128 * h, T.RT, 1 + h, LOW, [], "RT%d" % h)
         for h in range(2):
             count(128 * h, 128, T.RT, KB + h, ["RT%d" % h], "kb%d" % h)
+        ts(T.Ft[:, 0:512:2], T.iP[:], col(JB), None, A.is_equal, None, ["iP", "jb"], ["Ft0", "Ft1"])
+        quant("F", 0, 128, T.Ft[:], ["Ft0", "Ft1", "Fz"], ["F"])
         for h in range(2):
-            ts(T.Ft[:, h:512:4], T.iJ[:, 128 * h:128 * h + 128], col(JB), None, A.is_equal, None,
-               ["iJ", "jb"], ["Ft%d" % h])
-        quant("F", 0, 128, T.Ft[:], ["Ft0", "Ft1", "Fz2", "Fz3"], ["F"])
+            mm(3 + 2 * h, 128, "F", 0, "J", 128 * h, ["F", "J%d" % h])
+        if t == 0:
+            ts(T.pint[:, 4:5], T.pint[:, 0:1], 15, None, A.bitwise_and, None, ["pi0"], ["pi1"])
+            op("v", lambda: V.tensor_copy(col(PM), T.pint[:, 4:5]), ["pi1"], ["pm"])
         for h in range(2):
-            mm(3 + 2 * h, 128, "F", 0, "E", 128 * h, ["F", "E%d" % h])
-        for h in range(2):
-            ts(T.F2[:, 128 * h:128 * h + 128], T.iJ[:, 0:128], col(KB + h), 8.0, A.is_equal, A.mult,
-               ["iJ", "kb%d" % h], ["F2%d" % h])
-        for h in range(2):
-            op("v", lambda: V.tensor_tensor(T.Mt[:, h:512:4], T["ps%d" % (3 + 2 * h)][:, 0:128],
-                                            T.F2[:, 128 * h:128 * h + 128], A.mult),
-               ["ps%d" % (3 + 2 * h), "F2%d" % h], ["Mt%d" % h])
-        quant("M", 0, 128, T.Mt[:], ["Mt0", "Mt1", "Mz2", "Mz3"], ["M"])
+            ts(T.Mt[:, 2 * h:512:4], T["ps%d" % (3 + 2 * h)][:, 0:128], col(KB + h), 128.0, A.subtract, A.is_equal,
+               ["ps%d" % (3 + 2 * h), "kb%d" % h], ["Mt%d" % h])
+        quant("M", 0, 130, T.Mt[:], ["Mt0", "Mt1", "Ma", "Mb", "Mc", "Md"], ["M"])
         mm(0, 128, "C", 0, "M", 0, ["C", "M"])
-        mm(2, 128, "C", 256, "M", 0, ["C", "M"])
-        mm(1, 128, "C", 128, "M", 0, ["C", "M"])
-        mm(3, 128, "C", 384, "M", 0, ["C", "M"])
+        for h in range(2):
+            mm(2 + h, 130, "C", 128 + 128 * h, "M", 0, ["C", "M"])
         if t == 0:
             ts(T.A0[:], T.i16[:], col(PM), DROP + STEP, A.not_equal, A.mult, ["i16", "pm"], ["A0"])
-        op("v", lambda: V.tensor_tensor_scan(T.qq[:], T.Ct[:, 0:512:4], T.ps0[:, 0:128], 0.0, A.add, A.subtract),
-           ["ps0", "C00"], ["qq"])
-        op("v", lambda: V.tensor_tensor(T.key[:], T.qq[:], T.ps1[:, 0:128], A.add), ["ps1", "qq"], ["key"])
+        op("v", lambda: V.tensor_tensor_scan(T.qq[:], T.zer[:, 0:128], T.ps0[:, 0:128], 0.0, A.add, A.add),
+           ["ps0", "zer"], ["qq"])
+        op("v", lambda: V.tensor_tensor(T.key[:], T.qq[:], T.ps0[:, 0:128], A.mult), ["ps0", "qq"], ["key"])
         for h in range(2):
-            op("a", lambda: S.activation(T.Ut[:, 2 + h:512:4], T["ps%d" % (2 + h)][:, 0:128], F.Copy,
-                                         accum_out=col(CC + h)), ["ps%d" % (2 + h)], ["Ut%d" % (2 + h), "cc%d" % h])
+            op("a", lambda: S.activation(T.Ut[:, 2 * h + 1:520:4], T["ps%d" % (2 + h)][:, 0:130], F.Copy,
+                                         accum_out=col(CC + h)), ["ps%d" % (2 + h)], ["Us%d" % h, "cc%d" % h])
         if t == 0:
             op("a", lambda: S.activation(T.Am[:], T.A0[:], F.Identity, bias=-DROP), ["A0"], ["Am"])
         for h in range(2):
-            ts(T.Ut[:, h:512:4], T.key[:], col(CC + h), T.jc[:, h:h + 1], A.add, A.is_gt,
-               ["key", "cc%d" % h, "jc"], ["Ut%d" % h])
-        quant("U", 0, 128, T.Ut[:], ["Ut0", "Ut1", "Ut2", "Ut3"], ["U"])
+            ts(T.Ut[:, 2 * h:512:4], T.key[:], col(CC + h), T.qq[:, 127:128], A.subtract, A.is_le,
+               ["key", "cc%d" % h, "qq"], ["Ut%d" % h])
+        quant("U", 0, 128, T.Ut[:, 0:512], ["Ut0", "Ut1", "Us0", "Us1"], ["U"])
         mm(0, 128, "C", 0, "U", 0, ["C", "U"])
         if t == 0:
-            ts(col(CORR), col(PM), -STEP, 15 * STEP, A.mult, A.add, ["pm"], ["corr"])
+            ts(col(CORR), col(PM), -STEP, 15 * STEP - C_, A.mult, A.add, ["pm"], ["corr"])
         latch(0, 0, 0)
         ts(T[offa][:], T.D[:, 15:128:16], col(CORR), None, A.subtract, None, ["D0", "corr"], [offa])
-        pick(P, 0, tb, 256, offa, 0, 8, tw, P)
+        pick(P, 0, W, 256, offa, 0, 8, tw, P)
 
-        for kind, flip in (("q", 0), ("s", 1)):
-            parts = []
-            for h in range(2):
-                src = T[P + kind][:, H_ * h:H_ * h + H_]
-                dst = T[L + kind][:, H_ * rank:H_ * rank + H_]
-                if kind == "q":
-                    src, dst = src.bitcast(dt.uint8), dst.bitcast(dt.uint8)
-                parts.append((src, [(r, dst) for r in owners[h] if r != rank], halves[h ^ flip]))
-            send(parts, "p%d" % t, [P + kind])
+        for i, call in enumerate(_code_calls(T, topo, rank)):
+            send([(T[P + "q"][:, Q_ * u:Q_ * u + Q_].bitcast(dt.uint8),
+                   [(T.cores[r], T[L + "q"][:, Q_ * rank:Q_ * rank + Q_].bitcast(dt.uint8))], es)
+                  for u, r, es in call], "p%d" % t, [P + "q"])
+            if i == 0:
+                send([(T[P + "s"][:], [(c, T["H%d" % t][:]) for c, _ in _helpers(T, topo, rank)], home)], "h%d" % t,
+                     [P + "s"])
 
+        oq = Q_ // 16
+        pick(L, Q_ * rank, W, 256, offa, oq * me, oq * me + oq, tw, L + "o")
+        pick(L, NI, W, 256, offa, 0, 8 - oq, tw, L + "p")
+        op("a", lambda: S.activation(T.par[0:1, 128 * t:128 * t + 128], T.ps0[0:1, 0:128], F.Identity,
+                                     bias=float(C_)), ["ps0"], ["par%d" % t])
         if t == 0:
-            afill(T.Et[:, 1024:1536], 512, 0.0, ["Ez2"])
-            fill(T.Et[:, 1536:2048], 0.0, ["Ez3"])
-        if own:
-            h = own[0]
-            pick(L, H_ * rank, tb, 256, offa, 4 * h, 4 * h + 4, tw, L + "o")
-            pick(L, H_ * NR, tb, 256, offa, 4 * h, 4 * h + 4, tw, L + "p")
-        op("a", lambda: S.activation(T.par[0:1, 128 * t:128 * t + 128], T.ps0[0:1, 0:128], F.Copy),
-           ["ps0"], ["par%d" % t])
-        if t == 0:
-            make_e(2)
-            afill(T.Kt[:, 0:512], 512, 0.0, ["Kz0"])
-            afill(T.Kt[:, 512:1024], 512, 0.0, ["Kz1"])
-        if own:
-            afill(T.At[:, 0:256], 256, 0.0, ["Az0"])
-            afill(T.At[:, 512:768], 256, 0.0, ["Az1"])
+            fill(T.Et[:], 0.0, ["Ez"])
+            ts(col(G8), col(PM), float(NR), 1.0 - NI, A.is_ge, A.mult, ["pm"], ["g8"])
+            ts(T.Et[:, 3:515:4], T.dI[:], 0.0, 0.125, A.is_equal, A.mult, ["dI", "Ez"], ["Et"])
+            ts(col(IL), col(PM), float(Q_), col(G8), A.mult, A.add, ["pm", "g8"], ["il"])
+            for b in range(4):
+                quant("E", 128 * b, 128 * b + 128, T.Et[:, 3 - b:515 - b], ["Et"], ["E%d" % b])
+            ts(T.offi[:], T.c16[:], 0.125, col(IL), A.mult, A.add, ["c16", "il"], ["offi"])
+            afill(T.msk[:], NI, 1.0, ["msk"])
+            afill(T.msk[:, 0:NI:NR], Q_, 0.0, ["msk"])
+            for i in range(3):
+                afill(T.Kt[:, 1 + i:1024:4], 256, 0.0, ["Kz%d" % i])
+            afill(T.At[:, 256:512], 256, 0.0, ["Az"])
+            afill(T.At[:, 4 * Q_:256], 256 - 4 * Q_, 0.0, ["Ay"])
         dma("s", T.pa[t:t + 1, :], T.par[0:1, 128 * t:128 * t + 128], "out", ["par%d" % t], [])
         for h in range(2):
-            op("v", lambda: V.tensor_reduce(col(MU + h), T.Mt[:, h:512:4], AxisListType.X, A.add),
+            op("v", lambda: V.tensor_reduce(col(MU + h), T.Mt[:, 2 * h:512:4], AxisListType.X, A.add),
                ["Mt%d" % h], ["mu%d" % h])
         for h in range(2):
-            ts(T.Ft[:, h:512:4], T.iJ[:, 0:128], col(KB + h), col(MU + h), A.is_le, A.mult,
-               ["iJ", "kb%d" % h, "mu%d" % h], ["Ft%d" % h])
-        quant("F", 0, 128, T.Ft[:], ["Ft0", "Ft1", "Fz2", "Fz3"], ["F"])
-        mm(2, 256, "F", 0, "E", 0, ["F", "E0", "E1"])
-        ts(T.Kt[:, 0:1024:4], T.ps2[:, 0:256], 8.0, None, A.mult, None, ["ps2", "Kz0", "Kz1"], ["Kt"])
-        quant("K", 0, 256, T.Kt[:], ["Kt", "Kz0", "Kz1"], ["K"])
-
-        if own:
-            h = own[0]
-            arrives("p%d" % t, (NR - 1) * 2 * len(halves[0]), [L])
-            lk = [L, L + "oq", L + "os", L + "pq", L + "ps"]
-            for part in range(2):
-                for b in (1, 2, 3):
-                    mm(b - 1 + 4 * part, 256, "E", 128 * b, L, 256 * part, lk + ["E%d" % b])
-            for r in range(NR):
-                mm(3, 128, "E", 0, L, H_ * r, lk + ["E0"], r == 0, r == NR - 1)
-            steps = sorted((r + (b - 1), -b, r, b) for r in range(NR) for b in (1, 2, 3))
-            for _, _, r, b in steps:
-                ac = T.acc[:, H_ * (b - 1):H_ * b]
-                bank = "ps%d" % (b - 1 + 4 * (r // 4))
-                src = T[bank][:, H_ * (r % 4):H_ * (r % 4) + H_]
-                if r == 0 and b < 3:
-                    op("v", lambda: V.tensor_copy(ac, src), [bank], ["ac%d" % b])
-                elif r == 0:
-                    op("a", lambda: S.activation(ac, src, F.Copy), [bank], ["ac%d" % b])
-                elif r < NR - 1:
-                    op("v", lambda: V.tensor_tensor(ac, ac, src, A.add), [bank, "ac%d" % b], ["ac%d" % b])
-                else:
-                    op("v", lambda: V.tensor_tensor(T.At[:, 256 + b:512:4], ac, src, A.add),
-                       [bank, "ac%d" % b], ["At%d" % b])
-            op("a", lambda: S.activation(T.At[:, 256:512:4], T.ps3[:, 0:H_], F.Copy), ["ps3"], ["At0"])
-            ak = ["At0", "At1", "At2", "At3", "Az0", "Az1"]
-            quant(Aq, 0, 128, T.At[:, 256:768], ak, [Aq])
-            for kind in "qs":
-                src = T[Aq + kind][:, 0:H_]
-                dst = T[Bn + kind][:, H_ * (h + 1):H_ * (h + 2)]
-                if kind == "q":
-                    src, dst = src.bitcast(dt.uint8), dst.bitcast(dt.uint8)
-                send([(src, [(r, dst) for r in mine if r != rank], eng)], "b%d" % t, [Aq])
-        arrives("b%d" % t, (2 - len(own)) * 2 * len(eng), [Bn])
-
-        mm(1, 256, "C", 0, "K", 0, ["C", "K"])
-        for b in range(4):
-            mm(4 + b, 128, "E", 128 * b, P, 0, ["E%d" % b, P + "q", P + "s"], True, False)
-        if own:
-            quant(Bn, 128 * h, 128 * h + 128, T.At[:, 256 * h:256 * h + 512], ak, [Bn + "o"])
-        latch(0, 1, 0)
-        latch(128, 1, 128)
+            ts(T.Ft[:, 2 * h:512:4], T.iP[:, 0:256:2], col(KB + h), col(MU + h), A.is_le, A.mult,
+               ["iP", "kb%d" % h, "mu%d" % h], ["Ft%d" % h])
+        quant("F", 0, 128, T.Ft[:], ["Ft0", "Ft1", "Fz"], ["F"])
+        mm(2, 256, "F", 0, "J", 0, ["F", "J0", "J1"])
         if t == 0:
             ts(T.j16[:], T.c16[:], col(PM), None, A.add, None, ["c16", "pm"], ["j16"])
-        ts(T.z16[:], T.D[:, 15:256:16], col(CORR), None, A.subtract, None, ["D0", "D128", "corr"], ["z16"])
+        ts(T.Kt[:, 0:1024:4], T.ps2[:, 0:256], 128.0, -1.0, A.is_ge, A.mult, ["ps2"], ["Kt"])
+        quant("K", 0, 256, T.Kt[:], ["Kt", "Kz0", "Kz1", "Kz2"], ["K"])
+        mm(1, 256, "C", 0, "K", 0, ["C", "K"])
+
+        arrives("p%d" % t, landed, [L + "q"])
+        arrives("s%d" % t, (NR - 1) * ne, [L + "s"])
         if t == 0:
-            quant(W, 0, 256, T.xt[:], ["xt0", "xt1"], [W + "aq", W + "as"])
+            half = [(I, NI // 2 * h, L, NI, "offi", NI // 32 * h, NI // 32 * (h + 1), [L, L + "o"], I + "ab"[h])
+                    for h in range(2)]
+            pick(*half[0])
+            pick_codes(*half[1])
+            pick_scales("v", *half[1])
         else:
-            pw = "W%d" % (t - 1)
-            pick(W, 0, pw, 384, "offb%d" % (t - 1), 0, 16, [pw + "a", pw + "b"], W + "a")
-        ts(T.u16[:], T.z16[:], 0.0, C_ - 1.0, A.is_gt, A.mult, ["z16"], ["u16"])
+            pick(I, 0, L, NI, "offi", 0, NI // 16, [L, L + "o"], I + "a")
+        lk = [L + "q", L + "s", L + "oq", L + "os", L + "pq", L + "ps", "E0"]
+        for r in range(NR // 2):
+            mm(7, 128, "E", 0, L, Q_ * r, lk, r == 0, False)
+        for b in (1, 2, 3):
+            mm(3 + b, NI, "E", 128 * b, I, 0, [I + "aq", I + "as", I + "bq", I + "bs", "E%d" % b])
+        for r in range(NR // 2, NR):
+            mm(7, 128, "E", 0, L, Q_ * r, lk, False, r == NR - 1)
+        for b in (1, 2, 3):
+            z = T.Z[:, NI * (b - 1):NI * b]
+            op("v", lambda: V.tensor_tensor_scan(z, T.msk[:], T["ps%d" % (3 + b)][:, 0:NI], 0.0, A.mult, A.add),
+               ["ps%d" % (3 + b), "msk"], ["Z%d" % b])
+            zl = T.Z[:, NI * (b - 1) + NR - 1:NI * b:NR]
+            if b < 3:
+                op("a", lambda: S.activation(T.At[:, b:4 * Q_:4], zl, F.Copy), ["Z%d" % b], ["At%d" % b])
+            else:
+                op("a", lambda: S.activation(T.At[:, 0:4 * Q_:4], T.ps7[:, 0:Q_], F.Copy), ["ps7"], ["At0"])
+                op("v", lambda: V.tensor_copy(T.At[:, b:4 * Q_:4], zl), ["Z%d" % b], ["At%d" % b])
+        quant(Aq, 0, 128, T.At[:], ["At0", "At1", "At2", "At3", "Az", "Ay"], [Aq + "q", Aq + "s"])
+        for kind in "qs":
+            src = T[Aq + kind][:, 0:Q_]
+            dst = T[Bn + kind][:, Q_ * me:Q_ * me + Q_]
+            if kind == "q":
+                src, dst = src.bitcast(dt.uint8), dst.bitcast(dt.uint8)
+            send([(src, [(T.cores[r], dst) for r in peers], eng)], "b%d" % t, [Aq + kind])
+        arrives("b%d" % t, (nq - 1) * 2 * len(eng), [Bn])
+
+        for b in range(4):
+            mm(4 + b, 128, "E", 128 * b, P, 0, ["E%d" % b, P + "q", P + "s"], True, False)
+        if t == 0:
+            op("v", lambda: V.tensor_copy(T.offo[:], T.j16[:]), ["j16"], ["offo"])
+        pick(Bn, Q_ * me, Aq, 128, "offo", 0, oq, [Aq], Bn + "o")
+        latch(0, 1, 0)
+        latch(128, 1, 128)
+        ts(T.z16[:], T.D[:, 15:256:16], col(CORR), float(C_), A.subtract, A.subtract, ["D0", "D128", "corr"], ["z16"])
         if t == 0:
             quant("Ww", 0, 128, T.wt[:], ["wt"], ["Ww"])
+        ts(T.u16[:], T.z16[:], 0.0, C_ - 1.0, A.is_gt, A.mult, ["z16"], ["u16"])
         op("v", lambda: V.tensor_tensor(T.v16[:], T.u16[:], T.z16[:], A.add), ["u16", "z16"], ["v16"])
         op("v", lambda: V.tensor_tensor(T.w16[:], T.v16[:], T.j16[:], A.max), ["v16", "j16"], ["w16"])
         op("v", lambda: V.tensor_copy(T[offb][:], T.w16[:]), ["w16"], [offb])
 
-        bb, bo, bk = Bn, H_, [Bn, Bn + "o"]
+        bb, bk = Bn, [Bn, Bn + "oq", Bn + "os"]
         for b in range(4):
-            mm(4 + b, 128, "E", 128 * b, bb, bo, ["E%d" % b] + bk, False, True)
+            mm(4 + b, 128, "E", 128 * b, bb, 0, ["E%d" % b] + bk, False, True)
         last = t == R_ - 1
         if last:
-            mm(0, 128, "Ww", 0, bb, bo, ["Ww"] + bk)
+            mm(0, 128, "Ww", 0, bb, 0, ["Ww"] + bk)
         for b in range(4):
             src = T["ps%d" % (4 + b)][:, 0:128]
             if b % 2 == 1:
@@ -406,8 +457,9 @@ def rank_program(g, core, T, topo):
             dma("s", T.y[:, 256:384], T.ysb[:, 256:384], "out", ["yb"], [])
         quant(W, 256, 384, T.Vt[:], ["Vt0", "Vt1", "Vt2", "Vt3"], [W + "bq", W + "bs"])
         for h in range(2):
-            pick(Tn, 128 * h, W, 384, offb, 8 * h, 8 * h + 8, [W + "a", W + "b"], Tn + "%d" % h)
-        tb = Tn
+            pick(Wn, 128 * h, W, 384, offb, 8 * h, 8 * h + 8, tw + [W + "b"], Wn + "%d" % h)
+
+    tb = "W%d" % R_
 
     def scales_out(q, k):
         dma(q, T.osc[4 * k:4 * k + 4, :], T[tb + "s"][32 * k:32 * k + 4, :], "out", [tb + "0s", tb + "1s"], [])

@@ -1,5 +1,5 @@
 from concourse.bass import DstId, RemoteDMATransfer
-from concourse.mybir import dt, AluOpType, AxisListType, ActivationFunctionType
+from concourse.mybir import dt, AluOpType, ActivationFunctionType
 
 R_, C_, K_ = 2, 256, 128
 NR = 8
@@ -19,12 +19,11 @@ def _mx(name, n):
 
 
 for _n, _w in (("xt", 1024), ("bt", 512), ("wt", 512), ("Et", 520), ("Jt", 520), ("Ct", 1536), ("Ft", 512),
-               ("Mt", 520), ("Ut", 520), ("Kt", 1024), ("At", 512), ("Vt", 512), ("dI", 128), ("iP", 256),
-               ("i16", 128), ("zer", 256), ("junk", 256), ("key", 128), ("msk", NR * Q_), ("Z", 3 * NR * Q_)):
+               ("Mt", 520), ("nI", 130), ("Kt", 1024), ("At", 512), ("Vt", 512), ("dI", 130), ("ik", 128),
+               ("i16", 128), ("zer", 256), ("Zc", NR * Q_), ("msk", NR * Q_), ("Z", 3 * NR * Q_)):
     _sb(_n, _w, "bfloat16")
-for _n, _w in (("R", 256), ("RT", 256), ("qq", 128), ("Am", 128), ("A0", 128), ("D", 256), ("cols", 16),
-               ("ysb", 384), ("par", 256), ("c16", 16), ("j16", 16), ("z16", 16), ("u16", 16), ("v16", 16),
-               ("w16", 16)):
+for _n, _w in (("R", 256), ("RT", 256), ("below", 520), ("Am", 128), ("A0", 128), ("D", 256), ("cols", 16),
+               ("ysb", 384), ("par", 256), ("c16", 16), ("j16", 16), ("z16", 16), ("u16", 16)):
     _sb(_n, _w, "float32")
 _sb("pint", 8, "int32")
 _sb("offi", 16, "uint16")
@@ -35,7 +34,7 @@ for _n, _w in (("E", 512), ("J", 256), ("C", 384), ("Bb", 128), ("W%d" % R_, 256
 for _t in range(R_):
     _sb("offa%d" % _t, 8, "uint16")
     _sb("offb%d" % _t, 16, "uint16")
-    for _n, _w in (("P", 128), ("L", (NR - 1) * Q_ + 128), ("I", NR * Q_), ("A", 128), ("B", 128), ("W", 384)):
+    for _n, _w in (("L", NR * Q_ + K_), ("I", NR * Q_), ("A", 128), ("B", 128), ("W", 384)):
         _mx("%s%d" % (_n, _t), _w)
     _sb("H%d" % _t, K_, "uint8")
 for _i in range(8):
@@ -89,9 +88,10 @@ def _code_calls(T, topo, rank):
     other = [gr for gr in groups if gr is not mine][0]
     me, nq = mine.index(rank), len(mine)
     far = _engines(T, topo, T.cores[rank])[0]
-    turn = [(me + i) % nq for i in range(1, nq)]
-    calls = [[(u, mine[u]) for u in turn] + [(me, other[me])], [(u, other[u]) for u in turn[:2]],
-             [(turn[2], other[turn[2]])]]
+    near = [u for u in range(nq) if 2 * u // nq == 2 * me // nq and u != me]
+    away = [u for u in range(nq) if 2 * u // nq != 2 * me // nq]
+    calls = [[(u, gr[u]) for u in away for gr in (mine, other)], [(u, gr[u]) for u in near for gr in (mine, other)],
+             [(me, other[me])]]
     return [[(u, r, far[i * len(far) // len(call):(i + 1) * len(far) // len(call)]) for i, (u, r) in enumerate(call)]
             for call in calls]
 
@@ -215,8 +215,11 @@ def rank_program(g, core, T, topo):
     def fill(ap, val, wr):
         op("v", lambda: V.memset(ap, val), [], wr)
 
+    def act(out, in_, rd, wr, **kw):
+        op("a", lambda: S.activation(out, in_, F.Identity if "bias" in kw else F.Copy, **kw), rd, wr)
+
     def afill(ap, n, val, wr):
-        op("a", lambda: S.activation(ap, T.zer[:, 0:n], F.Identity, bias=val), ["zer"], wr)
+        act(ap, T.zer[:, 0:n], ["zer"], wr, bias=val)
 
     def iota(ap, pattern, base, cm, wr, small=True):
         if small:
@@ -231,7 +234,7 @@ def rank_program(g, core, T, topo):
 
     def col(i):
         return T.cols[:, i:i + 1]
-    JB, KB, CC, MU, PM, CORR, G8, IL = 0, 1, 3, 5, 7, 8, 9, 10
+    JB, KB, PC, HI, PM, CORR, G8, IL = 0, 2, 4, 5, 7, 8, 9, 10
 
     mine = [gr for gr in _planes(T, topo) if rank in gr][0]
     me = mine.index(rank)
@@ -246,32 +249,34 @@ def rank_program(g, core, T, topo):
     dma("s", T.xt[:, 512:1024], T.x[:, 512:1024], "ldx1", [], ["xt1"])
     dma("s", T.wt[:], T.w[:], "ldw", ["xt0", "xt1", "bt"], ["wt"])
 
-    iota(T.dI[:], [[1, 128]], 0, -1, ["dI"])
+    iota(T.dI[:], [[1, 130]], 0, -1, ["dI"])
     iota(T.pint[:, 0:1], [[0, 1]], 0, 1, ["pi0"], small=False)
-    iota(T.iP[:], [[1, 128], [128, 2]], 0, 0, ["iP"])
+    iota(col(PC), [[0, 1]], 0, 1, ["pc"])
+    iota(T.ik[:], [[1, 128]], 0, 0, ["ik"])
     iota(T.i16[:], [[0, 8], [1, 16]], 0, 0, ["i16"])
+    iota(T.Ct[:, 515:1536:4], [[0, 256]], 0, 0, ["Cc"])
+    iota(T.Ct[:, 513:1024:4], [[0, 128]], 1, 0, ["Cd"])
+    iota(T.Ct[:, 1025:1536:4], [[0, 128]], 0, 0, ["Ce"])
     iota(T.c16[:], [[16, 16]], 0, 0, ["c16"])
 
+    dg = T.dI[:, 0:128]
     fill(T.zer[:], 0.0, ["zer"])
     fill(T.Jt[:], 0.0, ["Jz"])
-    fill(T.Ct[:, 3:1536:4], 1.0, ["Ca"])
-    afill(T.Ct[:, 0:512:2], 256, -1.0, ["Cb"])
-    afill(T.Ct[:, 513:1536:4], 256, 0.0, ["Cd"])
-    afill(T.Ct[:, 1:512:4], 128, 1.0, ["Cc"])
-    afill(T.Ct[:, 514:1024:4], 128, 1.0, ["Ce"])
-    afill(T.Ct[:, 1024:1536:4], 128, 0.0, ["Cf"])
+    afill(T.Ct[:, 0:512:2], 256, -256.0, ["Ca"])
+    afill(T.Ct[:, 1:512:2], 256, -1.0, ["Cb"])
     afill(T.Ft[:, 1:512:2], 256, 1.0, ["Fz"])
-    afill(T.Mt[:, 1:512:4], 128, 1.0 / 128, ["Ma"])
-    afill(T.Mt[:, 3:512:4], 128, 0.0, ["Mb"])
-    afill(T.Mt[:, 512:520:2], 4, -0.5, ["Mc"])
-    afill(T.Mt[:, 513:520:2], 4, 0.5, ["Md"])
-    ts(T.Jt[:, 2:514:4], T.dI[:], 0.0, 128.0, A.is_equal, A.mult, ["dI", "Jz"], ["Ja"])
-    ts(T.Jt[:, 3:514:4], T.dI[:], 0.0, None, A.is_gt, None, ["dI", "Jz"], ["Jb"])
-    ts(T.Ct[:, 512:1024:4], T.dI[:], 0.0, None, A.is_lt, None, ["dI"], ["Cg"])
-    ts(T.Ct[:, 1026:1536:4], T.dI[:], 0.0, None, A.is_lt, None, ["dI"], ["Ch"])
+    afill(T.Mt[:, 512:520:2], 4, 0.0, ["Mz"])
+    ts(T.Jt[:, 2:514:4], dg, 0.0, 128.0, A.is_equal, A.mult, ["dI", "Jz"], ["Ja"])
+    ts(T.Jt[:, 3:514:4], dg, 0.0, None, A.is_gt, None, ["dI", "Jz"], ["Jb"])
+    ts(T.pint[:, 4:5], T.pint[:, 0:1], 15, None, A.bitwise_and, None, ["pi0"], ["pi1"])
+    ts(T.nI[:], T.dI[:], 0.0, -1.0, A.is_equal, A.mult, ["dI"], ["nI"])
+    op("v", lambda: V.tensor_copy(col(PM), T.pint[:, 4:5]), ["pi1"], ["pm"])
     for h in range(2):
         quant("J", 128 * h, 128 * h + 128, T.Jt[:, 2 - 2 * h:514 - 2 * h], ["Ja", "Jb"], ["J%d" % h])
-    quant("C", 0, 384, T.Ct[:], ["C" + c for c in "abcdefgh"], ["C"])
+    act(col(HI), col(PM), ["pm", "pc"], ["hi"], bias=col(PC), scale=-1.0)
+    act(T.Ct[:, 512:1024:2], T.Ft[:, 1:512:2], ["pm", "Fz"], ["Cf"], bias=col(PM))
+    act(T.Ct[:, 1024:1536:4], T.zer[:, 0:128], ["hi", "zer"], ["Cg"], bias=col(HI))
+    act(T.Ct[:, 1026:1536:4], T.Ct[:, 1024:1536:4], ["Cg"], ["Ch"], bias=128.0)
 
     quant("Bb", 0, 128, T.bt[:], ["bt"], ["Bb"])
     for h in range(2):
@@ -283,8 +288,8 @@ def rank_program(g, core, T, topo):
                                              A.max, A.add), ["ps%d" % bank, "zer"] + rd, [tag])
 
     def count(lo, n, src, cnt, rd, ctag):
-        op("a", lambda: S.activation(T.junk[:, 0:n], src[:, lo:lo + n], F.Sign, bias=src[:, lo + n - 1:lo + n],
-                                     scale=-1.0, accum_out=col(cnt)), rd, [ctag, "junk"])
+        op("a", lambda: S.activation(T.below[:, 130 * cnt:130 * cnt + n], src[:, lo:lo + n], F.Sign,
+                                     bias=src[:, lo + n - 1:lo + n], scale=-1.0, accum_out=col(cnt)), rd, [ctag])
 
     def latch(lo, bank, plo):
         op("v", lambda: V.tensor_tensor_scan(T.D[:, lo:lo + 128], T.Am[:], T["ps%d" % bank][:, plo:plo + 128], 0.0,
@@ -298,123 +303,127 @@ def rank_program(g, core, T, topo):
         Wn = "W%d" % (t + 1)
         th = [[W + "%dq" % h, W + "%ds" % h] for h in range(2)]
         tw = [W + "0", W + "1"]
+        pk = [P + "0q", P + "0s", P + "1q", P + "1s"]
         offa, offb = "offa%d" % t, "offb%d" % t
 
-        mm(0, 128, bb, 0, W, 0, th[0] + bk)
-        mm(4, 128, bb, 0, W, 128, th[1] + bk)
-        mm(1, 128, W, 0, bb, 0, th[0] + bk)
-        mm(2, 128, W, 128, bb, 0, th[1] + bk)
-        running_max(0, T.R, 0, LOW, [], "R0")
-        running_max(128, T.R, 4, T.R[:, 127:128], ["R0"], "R1")
-        count(0, 256, T.R, JB, ["R0", "R1"], "jb")
         for h in range(2):
+            mm(4 * h, 128, bb, 0, W, 128 * h, th[h] + bk)
+            mm(1 + h, 128, W, 128 * h, bb, 0, th[h] + bk)
+        for h in range(2):
+            running_max(128 * h, T.R, 4 * h, T.R[:, 127:128] if h else LOW, ["R0"] if h else [], "R%d" % h)
             running_max(128 * h, T.RT, 1 + h, LOW, [], "RT%d" % h)
+        count(0, 128, T.R, JB, ["R0"], "jb0")
+        count(127, 129, T.R, JB + 1, ["R0", "R1"], "jb1")
         for h in range(2):
             count(128 * h, 128, T.RT, KB + h, ["RT%d" % h], "kb%d" % h)
-        ts(T.Ft[:, 0:512:2], T.iP[:], col(JB), None, A.is_equal, None, ["iP", "jb"], ["Ft0", "Ft1"])
+        if t == 0:
+            quant("C", 0, 128, T.Ct[:, 0:512], ["Ca", "Cb"], ["C0"])
+        ts(T.Ft[:, 2:512:4], T.ik[:], col(JB + 1), -1.0, A.subtract, A.is_equal, ["ik", "jb1"], ["Ft1"])
+        ts(T.Ft[:, 0:512:4], T.ik[:], col(JB), T.below[:, 130:131], A.is_equal, A.is_gt, ["ik", "jb0", "jb1"], ["Ft0"])
         quant("F", 0, 128, T.Ft[:], ["Ft0", "Ft1", "Fz"], ["F"])
         for h in range(2):
             mm(3 + 2 * h, 128, "F", 0, "J", 128 * h, ["F", "J%d" % h])
         if t == 0:
-            ts(T.pint[:, 4:5], T.pint[:, 0:1], 15, None, A.bitwise_and, None, ["pi0"], ["pi1"])
-            op("v", lambda: V.tensor_copy(col(PM), T.pint[:, 4:5]), ["pi1"], ["pm"])
+            ts(T.A0[:], T.i16[:], col(PM), DROP + STEP, A.not_equal, A.mult, ["i16", "pm"], ["A0"])
         for h in range(2):
             ts(T.Mt[:, 2 * h:512:4], T["ps%d" % (3 + 2 * h)][:, 0:128], col(KB + h), 128.0, A.subtract, A.is_equal,
                ["ps%d" % (3 + 2 * h), "kb%d" % h], ["Mt%d" % h])
-        quant("M", 0, 130, T.Mt[:], ["Mt0", "Mt1", "Ma", "Mb", "Mc", "Md"], ["M"])
-        mm(0, 128, "C", 0, "M", 0, ["C", "M"])
-        for h in range(2):
-            mm(2 + h, 130, "C", 128 + 128 * h, "M", 0, ["C", "M"])
+        for h, more in ((0, "zer"), (1, "nI")):
+            op("v", lambda: V.tensor_tensor_scan(T.Mt[:, 2 * h + 1:520:4], T.Mt[:, 2 * h:520:4], T[more][:, 0:130],
+                                                 0.0, A.add, A.add), ["Mt%d" % h, "Mz", more], ["N%d" % h])
+        quant("M", 0, 130, T.Mt[:], ["Mt0", "Mt1", "N0", "N1", "Mz"], ["M"])
+        mm(2, 130, "J", 0, "M", 0, ["J0", "M"])
+        mm(0, 128, "C", 0, "M", 0, ["C0", "M"])
         if t == 0:
-            ts(T.A0[:], T.i16[:], col(PM), DROP + STEP, A.not_equal, A.mult, ["i16", "pm"], ["A0"])
-        op("v", lambda: V.tensor_tensor_scan(T.qq[:], T.zer[:, 0:128], T.ps0[:, 0:128], 0.0, A.add, A.add),
-           ["ps0", "zer"], ["qq"])
-        op("v", lambda: V.tensor_tensor(T.key[:], T.qq[:], T.ps0[:, 0:128], A.mult), ["ps0", "qq"], ["key"])
-        for h in range(2):
-            op("a", lambda: S.activation(T.Ut[:, 2 * h + 1:520:4], T["ps%d" % (2 + h)][:, 0:130], F.Copy,
-                                         accum_out=col(CC + h)), ["ps%d" % (2 + h)], ["Us%d" % h, "cc%d" % h])
+            quant("C", 128, 384, T.Ct[:, 512:1536], ["C" + c for c in "cdefgh"], ["C1"])
+            act(T.Am[:], T.A0[:], ["A0"], ["Am"], bias=-DROP)
+        mm(6, 128, "C", 256, "M", 0, ["C1", "M"], True, False)
+        ts(T.Mt[:, 1:512:4], T.ps0[:, 0:128], T.ps2[:, 128:129], col(PC), A.add, A.is_gt, ["ps0", "ps2", "pc"], ["N0"])
+        quant("U", 0, 128, T.Mt[:, 0:512], ["Mt0", "Mt1", "N0", "N1"], ["U"])
+        mm(6, 128, "C", 128, "U", 0, ["C1", "U"], False, True)
         if t == 0:
-            op("a", lambda: S.activation(T.Am[:], T.A0[:], F.Identity, bias=-DROP), ["A0"], ["Am"])
-        for h in range(2):
-            ts(T.Ut[:, 2 * h:512:4], T.key[:], col(CC + h), T.qq[:, 127:128], A.subtract, A.is_le,
-               ["key", "cc%d" % h, "qq"], ["Ut%d" % h])
-        quant("U", 0, 128, T.Ut[:, 0:512], ["Ut0", "Ut1", "Us0", "Us1"], ["U"])
-        mm(0, 128, "C", 0, "U", 0, ["C", "U"])
-        if t == 0:
-            ts(col(CORR), col(PM), -STEP, 15 * STEP - C_, A.mult, A.add, ["pm"], ["corr"])
-        latch(0, 0, 0)
+            ts(col(CORR), col(PM), -STEP, 15 * STEP + 1.0, A.mult, A.add, ["pm"], ["corr"])
+        latch(0, 6, 0)
         ts(T[offa][:], T.D[:, 15:128:16], col(CORR), None, A.subtract, None, ["D0", "corr"], [offa])
-        pick(P, 0, W, 256, offa, 0, 8, tw, P)
+        for h in (1 - 2 * me // nq, 2 * me // nq):
+            pick(L, NI + 64 * h, W, 256, offa, 4 * h, 4 * h + 4, tw, P + "%d" % h)
 
         for i, call in enumerate(_code_calls(T, topo, rank)):
-            send([(T[P + "q"][:, Q_ * u:Q_ * u + Q_].bitcast(dt.uint8),
+            send([(T[L + "q"][:, NI + Q_ * u:NI + Q_ * u + Q_].bitcast(dt.uint8),
                    [(T.cores[r], T[L + "q"][:, Q_ * rank:Q_ * rank + Q_].bitcast(dt.uint8))], es)
-                  for u, r, es in call], "p%d" % t, [P + "q"])
+                  for u, r, es in call], "p%d" % t, [P + "%dq" % (2 * u // nq) for u, _, _ in call])
             if i == 0:
-                send([(T[P + "s"][:], [(c, T["H%d" % t][:]) for c, _ in _helpers(T, topo, rank)], home)], "h%d" % t,
-                     [P + "s"])
+                send([(T[L + "s"][:, NI:NI + K_], [(c, T["H%d" % t][:]) for c, _ in _helpers(T, topo, rank)], home)],
+                     "h%d" % t, [P + "0s", P + "1s"])
 
         oq = Q_ // 16
         pick(L, Q_ * rank, W, 256, offa, oq * me, oq * me + oq, tw, L + "o")
-        pick(L, NI, W, 256, offa, 0, 8 - oq, tw, L + "p")
-        op("a", lambda: S.activation(T.par[0:1, 128 * t:128 * t + 128], T.ps0[0:1, 0:128], F.Identity,
-                                     bias=float(C_)), ["ps0"], ["par%d" % t])
+        act(T.par[0:1, 128 * t:128 * t + 128], T.ps6[0:1, 0:128], ["ps6"], ["par%d" % t], bias=-1.0)
         if t == 0:
             fill(T.Et[:], 0.0, ["Ez"])
             ts(col(G8), col(PM), float(NR), 1.0 - NI, A.is_ge, A.mult, ["pm"], ["g8"])
-            ts(T.Et[:, 3:515:4], T.dI[:], 0.0, 0.125, A.is_equal, A.mult, ["dI", "Ez"], ["Et"])
+            ts(T.Et[:, 3:515:4], dg, 0.0, 0.125, A.is_equal, A.mult, ["dI", "Ez"], ["Et"])
             ts(col(IL), col(PM), float(Q_), col(G8), A.mult, A.add, ["pm", "g8"], ["il"])
             for b in range(4):
                 quant("E", 128 * b, 128 * b + 128, T.Et[:, 3 - b:515 - b], ["Et"], ["E%d" % b])
             ts(T.offi[:], T.c16[:], 0.125, col(IL), A.mult, A.add, ["c16", "il"], ["offi"])
             afill(T.msk[:], NI, 1.0, ["msk"])
             afill(T.msk[:, 0:NI:NR], Q_, 0.0, ["msk"])
-            for i in range(3):
-                afill(T.Kt[:, 1 + i:1024:4], 256, 0.0, ["Kz%d" % i])
+            for i in (0, 3):
+                afill(T.Kt[:, i:1024:4], 256, 0.0, ["Kz%d" % i])
             afill(T.At[:, 256:512], 256, 0.0, ["Az"])
             afill(T.At[:, 4 * Q_:256], 256 - 4 * Q_, 0.0, ["Ay"])
         dma("s", T.pa[t:t + 1, :], T.par[0:1, 128 * t:128 * t + 128], "out", ["par%d" % t], [])
+        mm(2, 384, "M", 0, "E", 0, ["M", "E0", "E1", "E2"])
         for h in range(2):
-            op("v", lambda: V.tensor_reduce(col(MU + h), T.Mt[:, 2 * h:512:4], AxisListType.X, A.add),
-               ["Mt%d" % h], ["mu%d" % h])
-        for h in range(2):
-            ts(T.Ft[:, 2 * h:512:4], T.iP[:, 0:256:2], col(KB + h), col(MU + h), A.is_le, A.mult,
-               ["iP", "kb%d" % h, "mu%d" % h], ["Ft%d" % h])
-        quant("F", 0, 128, T.Ft[:], ["Ft0", "Ft1", "Fz"], ["F"])
-        mm(2, 256, "F", 0, "J", 0, ["F", "J0", "J1"])
+            for slot, size in ((2, 8.0), (1, 1024.0)):
+                act(T.Kt[:, 512 * h + slot:512 * h + 512:4], T.ps2[:, 256 * h:256 * h + 128], ["ps2"],
+                    ["K%d%d" % (h, slot)], scale=size)
         if t == 0:
             ts(T.j16[:], T.c16[:], col(PM), None, A.add, None, ["c16", "pm"], ["j16"])
-        ts(T.Kt[:, 0:1024:4], T.ps2[:, 0:256], 128.0, -1.0, A.is_ge, A.mult, ["ps2"], ["Kt"])
-        quant("K", 0, 256, T.Kt[:], ["Kt", "Kz0", "Kz1", "Kz2"], ["K"])
-        mm(1, 256, "C", 0, "K", 0, ["C", "K"])
+            op("v", lambda: V.tensor_copy(T.offo[:], T.j16[:]), ["j16"], ["offo"])
+            ts(T.u16[:], T.j16[:], col(CORR), None, A.add, None, ["j16", "corr"], ["u16"])
+        quant("K", 0, 256, T.Kt[:], ["K01", "K02", "K11", "K12", "Kz0", "Kz3"], ["K"])
+        mm(1, 256, "C", 256, "K", 0, ["C1", "K"], True, False)
+        mm(1, 256, "C", 128, "K", 0, ["C1", "K"], False, True)
 
         arrives("p%d" % t, landed, [L + "q"])
         arrives("s%d" % t, (NR - 1) * ne, [L + "s"])
-        if t == 0:
-            half = [(I, NI // 2 * h, L, NI, "offi", NI // 32 * h, NI // 32 * (h + 1), [L, L + "o"], I + "ab"[h])
-                    for h in range(2)]
-            pick(*half[0])
-            pick_codes(*half[1])
-            pick_scales("v", *half[1])
-        else:
-            pick(I, 0, L, NI, "offi", 0, NI // 16, [L, L + "o"], I + "a")
-        lk = [L + "q", L + "s", L + "oq", L + "os", L + "pq", L + "ps", "E0"]
-        for r in range(NR // 2):
+        ni = 4 if t == 0 else 2
+        part = [(I, NI // ni * i, L, NI, "offi", NI // 16 // ni * i, NI // 16 // ni * (i + 1), [L, L + "o"],
+                 I + "%d" % i) for i in range(ni)]
+        for p in part:
+            pick_codes(*p)
+        for i, p in enumerate(part):
+            pick_scales("v" if t == 0 and i % 2 else "a", *p)
+        ik = [[I + "%d%s" % (i, k) for i in range(ni // 2 * h, ni // 2 * (h + 1)) for k in "qs"] for h in range(2)]
+        lk = [L + "q", L + "s", L + "oq", L + "os", "E0"] + pk
+        bank = {(1, 0): 4, (3, 0): 6, (2, 0): 5, (1, 1): 3, (2, 1): 0, (3, 1): 2}
+        for r in range(3):
             mm(7, 128, "E", 0, L, Q_ * r, lk, r == 0, False)
-        for b in (1, 2, 3):
-            mm(3 + b, NI, "E", 128 * b, I, 0, [I + "aq", I + "as", I + "bq", I + "bs", "E%d" % b])
-        for r in range(NR // 2, NR):
+        for (b, h), k in bank.items():
+            mm(k, 128, "E", 128 * b, I, 128 * h, ik[h] + ["E%d" % b])
+        for r in range(3, NR):
             mm(7, 128, "E", 0, L, Q_ * r, lk, False, r == NR - 1)
-        for b in (1, 2, 3):
-            z = T.Z[:, NI * (b - 1):NI * b]
-            op("v", lambda: V.tensor_tensor_scan(z, T.msk[:], T["ps%d" % (3 + b)][:, 0:NI], 0.0, A.mult, A.add),
-               ["ps%d" % (3 + b), "msk"], ["Z%d" % b])
-            zl = T.Z[:, NI * (b - 1) + NR - 1:NI * b:NR]
-            if b < 3:
-                op("a", lambda: S.activation(T.At[:, b:4 * Q_:4], zl, F.Copy), ["Z%d" % b], ["At%d" % b])
-            else:
-                op("a", lambda: S.activation(T.At[:, 0:4 * Q_:4], T.ps7[:, 0:Q_], F.Copy), ["ps7"], ["At0"])
-                op("v", lambda: V.tensor_copy(T.At[:, b:4 * Q_:4], zl), ["Z%d" % b], ["At%d" % b])
+
+        def add_up(lo, n, src, rd, tag):
+            op("v", lambda: V.tensor_tensor_scan(T.Z[:, lo:lo + n], T.msk[:, 0:n], src, 0.0, A.mult, A.add),
+               rd + ["msk"], [tag])
+
+        def sums(b):
+            return T.Z[:, NI * (b - 1) + NR - 1:NI * b:NR]
+        for h in range(2):
+            for b in (1, 3):
+                k = "ps%d" % bank[b, h]
+                add_up(NI * (b - 1) + 128 * h, 128, T[k][:, 0:128], [k], "Z%d%d" % (b, h))
+        for h in range(2):
+            k = "ps%d" % bank[2, h]
+            act(T.Zc[:, 128 * h:128 * h + 128], T[k][:, 0:128], [k], ["Zc%d" % h])
+        add_up(NI, NI, T.Zc[:], ["Zc0", "Zc1"], "Z2")
+        act(T.At[:, 1:4 * Q_:4], sums(1), ["Z10", "Z11"], ["At1"])
+        act(T.At[:, 3:4 * Q_:4], sums(3), ["Z30", "Z31"], ["At3"])
+        act(T.At[:, 0:4 * Q_:4], T.ps7[:, 0:Q_], ["ps7"], ["At0"])
+        op("v", lambda: V.tensor_copy(T.At[:, 2:4 * Q_:4], sums(2)), ["Z2"], ["At2"])
         quant(Aq, 0, 128, T.At[:], ["At0", "At1", "At2", "At3", "Az", "Ay"], [Aq + "q", Aq + "s"])
         for kind in "qs":
             src = T[Aq + kind][:, 0:Q_]
@@ -425,19 +434,14 @@ def rank_program(g, core, T, topo):
         arrives("b%d" % t, (nq - 1) * 2 * len(eng), [Bn])
 
         for b in range(4):
-            mm(4 + b, 128, "E", 128 * b, P, 0, ["E%d" % b, P + "q", P + "s"], True, False)
-        if t == 0:
-            op("v", lambda: V.tensor_copy(T.offo[:], T.j16[:]), ["j16"], ["offo"])
+            mm(4 + b, 128, "E", 128 * b, L, NI, ["E%d" % b] + pk, True, False)
         pick(Bn, Q_ * me, Aq, 128, "offo", 0, oq, [Aq], Bn + "o")
         latch(0, 1, 0)
         latch(128, 1, 128)
-        ts(T.z16[:], T.D[:, 15:256:16], col(CORR), float(C_), A.subtract, A.subtract, ["D0", "D128", "corr"], ["z16"])
         if t == 0:
             quant("Ww", 0, 128, T.wt[:], ["wt"], ["Ww"])
-        ts(T.u16[:], T.z16[:], 0.0, C_ - 1.0, A.is_gt, A.mult, ["z16"], ["u16"])
-        op("v", lambda: V.tensor_tensor(T.v16[:], T.u16[:], T.z16[:], A.add), ["u16", "z16"], ["v16"])
-        op("v", lambda: V.tensor_tensor(T.w16[:], T.v16[:], T.j16[:], A.max), ["v16", "j16"], ["w16"])
-        op("v", lambda: V.tensor_copy(T[offb][:], T.w16[:]), ["w16"], [offb])
+        op("v", lambda: V.tensor_tensor(T.z16[:], T.D[:, 15:256:16], T.u16[:], A.max), ["D0", "D128", "u16"], ["z16"])
+        ts(T[offb][:], T.z16[:], col(CORR), None, A.subtract, None, ["z16", "corr"], [offb])
 
         bb, bk = Bn, [Bn, Bn + "oq", Bn + "os"]
         for b in range(4):
@@ -450,10 +454,9 @@ def rank_program(g, core, T, topo):
             if b % 2 == 1:
                 ts(T.Vt[:, b:512:4], src, 4.0, None, A.mult, None, ["ps%d" % (4 + b)], ["Vt%d" % b])
             else:
-                op("a", lambda: S.activation(T.Vt[:, b:512:4], src, F.Copy, scale=4.0),
-                   ["ps%d" % (4 + b)], ["Vt%d" % b])
+                act(T.Vt[:, b:512:4], src, ["ps%d" % (4 + b)], ["Vt%d" % b], scale=4.0)
         if last:
-            op("a", lambda: S.activation(T.ysb[:, 256:384], T.ps0[:, 0:128], F.Copy), ["ps0"], ["yb"])
+            act(T.ysb[:, 256:384], T.ps0[:, 0:128], ["ps0"], ["yb"])
             dma("s", T.y[:, 256:384], T.ysb[:, 256:384], "out", ["yb"], [])
         quant(W, 256, 384, T.Vt[:], ["Vt0", "Vt1", "Vt2", "Vt3"], [W + "bq", W + "bs"])
         for h in range(2):

from concourse.bass import DstId, RemoteDMATransfer
from concourse.mybir import dt, AluOpType, ActivationFunctionType

R_, C_, K_ = 2, 256, 128
NR = 8
Q_ = 32
STEP, DROP = 512.0, 16384.0

SCRATCH = {}


def _sb(name, n, dtype):
    SCRATCH[name] = ("sbuf", [128, n], dtype)


def _mx(name, n):
    _sb(name + "q", n, "float8_e4m3fn_x4")
    _sb(name + "s", n, "uint8")


for _n, _w in (("xt", 1024), ("bt", 512), ("wt", 512), ("Et", 520), ("Jt", 520), ("Ct", 1536), ("Ft", 512),
               ("Mt", 520), ("nI", 130), ("Kt", 1024), ("At", 512), ("Vt", 512), ("dI", 130), ("ik", 128),
               ("i16", 128), ("zer", 256), ("Zc", NR * Q_), ("msk", NR * Q_), ("Z", 3 * NR * Q_)):
    _sb(_n, _w, "bfloat16")
for _n, _w in (("R", 256), ("RT", 256), ("below", 520), ("Am", 128), ("A0", 128), ("D", 256), ("cols", 16),
               ("ysb", 384), ("par", 256), ("c16", 16), ("j16", 16), ("z16", 16), ("u16", 16)):
    _sb(_n, _w, "float32")
_sb("pint", 8, "int32")
_sb("offi", 16, "uint16")
_sb("offo", 16, "uint16")
for _n, _w in (("E", 512), ("J", 256), ("C", 384), ("Bb", 128), ("W%d" % R_, 256), ("Ww", 128), ("F", 128),
               ("M", 130), ("U", 128), ("K", 256)):
    _mx(_n, _w)
for _t in range(R_):
    _sb("offa%d" % _t, 8, "uint16")
    _sb("offb%d" % _t, 16, "uint16")
    for _n, _w in (("L", NR * Q_ + K_), ("I", NR * Q_), ("A", 128), ("B", 128), ("W", 384)):
        _mx("%s%d" % (_n, _t), _w)
    _sb("H%d" % _t, K_, "uint8")
for _i in range(8):
    SCRATCH["ps%d" % _i] = ("psum", [128, 512], "float32")

SEMAPHORES = ["cv", "ca", "ct", "cg", "ldx0", "ldx1", "ldb", "ldw", "out", "sent", "p0", "p1", "b0", "b1",
              "h0", "h1", "s0", "s1"]


def _planes(T, topo):
    groups = []
    for r, c in enumerate(T.cores):
        for gr in groups:
            if topo.same_plane(topo.chip(T.cores[gr[0]]), topo.chip(c)):
                gr.append(r)
                break
        else:
            groups.append([r])
    return groups


def _helpers(T, topo, rank):
    core = T.cores[rank]
    near = sorted((c for c in topo.cores_of(core) if c not in T.cores), key=lambda c: topo.die(c) != topo.die(core))
    found = []
    for gr in sorted(_planes(T, topo), key=lambda gr: rank in gr):
        c = [c for c in near if c not in [f for f, _ in found] and all(topo.may_write(c, T.cores[r]) for r in gr)][0]
        found.append((c, gr))
    return found


def _write(T, topo, src, dsts, eng, sem):
    ids = []
    for c, _ in dsts:
        rid, pid, _e = topo.addr(c)
        ids.append(DstId(rid=rid, pnc=pid))
    return RemoteDMATransfer(dst_ids=ids, dma_engine_mask=sum(1 << e for e in eng), remote_sem=T.sem[sem], src=src,
                             dsts=[d for _, d in dsts])


def _engines(T, topo, core):
    beside = topo.engines(core, [c for c in topo.cores_of(core) if c != core][0])
    off = [c for c in T.cores if topo.chip(c) != topo.chip(core)]
    far = [e for e in beside if all(e in topo.engines(core, c) for c in off)]
    return far, [e for e in beside if e not in far]


def _code_calls(T, topo, rank):
    groups = _planes(T, topo)
    mine = [gr for gr in groups if rank in gr][0]
    other = [gr for gr in groups if gr is not mine][0]
    me, nq = mine.index(rank), len(mine)
    far = _engines(T, topo, T.cores[rank])[0]
    near = [u for u in range(nq) if 2 * u // nq == 2 * me // nq and u != me]
    away = [u for u in range(nq) if 2 * u // nq != 2 * me // nq]
    calls = [[(u, gr[u]) for u in away for gr in (mine, other)], [(u, gr[u]) for u in near for gr in (mine, other)],
             [(me, other[me])]]
    return [[(u, r, far[i * len(far) // len(call):(i + 1) * len(far) // len(call)]) for i, (u, r) in enumerate(call)]
            for call in calls]


def _hand_on(g, core, T, topo):
    for rank in range(NR):
        for c, gr in _helpers(T, topo, rank):
            if c != core:
                continue
            far = _engines(T, topo, core)[0]
            home = _engines(T, topo, T.cores[rank])[1]
            ne = len(far) // len(gr)
            sent = 0
            for t in range(R_):
                g.wait_ge(T.sem["h%d" % t], len(home))
                trs = [_write(T, topo, T["H%d" % t][:, Q_ * u:Q_ * u + Q_],
                              [(T.cores[r], T["L%ds" % t][:, Q_ * rank:Q_ * rank + Q_])], far[ne * u:ne * u + ne],
                              "s%d" % t) for u, r in enumerate(gr) if r != rank]
                g.remote_dma_fused(trs, local_sem=T.sem.sent)
                sent += ne * len(trs)
            g.wait_ge(T.sem.sent, sent)


def rank_program(g, core, T, topo):
    rank = T.rank_of(core)
    if rank is None:
        _hand_on(g, core, T, topo)
        return
    A = AluOpType
    F = ActivationFunctionType
    V, S, PE = g.vector, g.scalar, g.tensor
    queue = {"v": V, "a": S, "t": PE, "g": g, "s": g.sync}
    csem = {"v": "cv", "a": "ca", "t": "ct", "g": "cg"}
    total = {n: 0 for n in SEMAPHORES}
    known = {q: {} for q in queue}
    lastw, readers = {}, {}

    def need(q, evs):
        want = {}
        for ev in evs:
            if ev[3] == "t" and q == "t":
                continue
            if known[q].get(ev[0], 0) < ev[1] and (ev[0] not in want or want[ev[0]][1] < ev[1]):
                want[ev[0]] = ev
        for ev in sorted(want.values(), key=lambda e: e[3] == q):
            if known[q].get(ev[0], 0) >= ev[1]:
                continue
            queue[q].wait_ge(T.sem[ev[0]], ev[1])
            known[q][ev[0]] = ev[1]
            for s, n in ev[2].items():
                if known[q].get(s, 0) < n:
                    known[q][s] = n

    def deps(q, rd, wr):
        evs = []
        for k in rd:
            if k in lastw:
                evs.append(lastw[k])
            if k.startswith("ps"):
                evs += [e for e in readers.get(k, []) if e[3] != q]
        for k in wr:
            if k in lastw:
                evs.append(lastw[k])
            evs += readers.get(k, [])
        need(q, evs)

    def note(ev, rd, wr):
        for k in rd:
            readers.setdefault(k, []).append(ev)
        for k in wr:
            lastw[k] = ev
            readers[k] = []

    def op(q, fn, rd, wr):
        deps(q, rd, wr)
        s = csem[q]
        total[s] += 1
        fn().then_inc(T.sem[s], 1)
        note((s, total[s], dict(known[q]), q), rd, wr)

    def dma(q, out, in_, sem, rd, wr):
        deps(q, rd, wr)
        total[sem] += 16
        queue[q].dma_start(out, in_).then_inc(T.sem[sem], 16)
        note((sem, total[sem], dict(known[q]), "dma"), [], wr)

    def arrives(sem, n, keys):
        total[sem] = n
        for k in keys:
            lastw[k] = (sem, n, {}, "far")

    def quant(name, a, b, tile, rd, wr):
        op("v", lambda: V.quantize_mx(T[name + "q"][:, a:b], T[name + "s"][:, a:b], tile), rd, wr)

    def mm(bank, n, w, wa, x, xa, rd, start=True, stop=True):
        op("t", lambda: PE.matmul_mx(T["ps%d" % bank][:, 0:n], T[w + "q"][:, wa:wa + 128], T[w + "s"][:, wa:wa + 128],
                                     T[x + "q"][:, xa:xa + n], T[x + "s"][:, xa:xa + n], start, stop),
           rd, ["ps%d" % bank])

    def pick_codes(dst, da, src, sn, off, oa, ob, rd, key):
        n = 16 * (ob - oa)
        op("v", lambda: V.tensor_copy(T[dst + "q"][:, da:da + n].bitcast(dt.uint32),
                                      T[src + "q"][:, 0:sn].bitcast(dt.uint32).indirect(T[off][:, oa:ob])),
           [k + "q" for k in rd] + [off], [key + "q"])

    def pick_scales(q, dst, da, src, sn, off, oa, ob, rd, key):
        out, win = T[dst + "s"][:, da:da + 16 * (ob - oa)], T[src + "s"][:, 0:sn].indirect(T[off][:, oa:ob])
        op(q, (lambda: S.activation(out, win, F.Copy)) if q == "a" else (lambda: V.tensor_copy(out, win)),
           [k + "s" for k in rd] + [off], [key + "s"])

    def pick(*args):
        pick_codes(*args)
        pick_scales("a", *args)

    def ts(out, in0, s1, s2, op0, op1, rd, wr):
        if op1 is None:
            op("v", lambda: V.tensor_scalar(out, in0, s1, None, op0), rd, wr)
        else:
            op("v", lambda: V.tensor_scalar(out, in0, s1, s2, op0, op1), rd, wr)

    def fill(ap, val, wr):
        op("v", lambda: V.memset(ap, val), [], wr)

    def act(out, in_, rd, wr, **kw):
        op("a", lambda: S.activation(out, in_, F.Identity if "bias" in kw else F.Copy, **kw), rd, wr)

    def afill(ap, n, val, wr):
        act(ap, T.zer[:, 0:n], ["zer"], wr, bias=val)

    def iota(ap, pattern, base, cm, wr, small=True):
        if small:
            op("g", lambda: g.iota(ap, pattern, base, cm, allow_small_or_imprecise_dtypes=True), [], wr)
        else:
            op("g", lambda: g.iota(ap, pattern, base, cm), [], wr)

    def send(parts, sem, rd):
        deps("g", rd, [])
        g.remote_dma_fused([_write(T, topo, src, dsts, es, sem) for src, dsts, es in parts], local_sem=T.sem.sent)
        total["sent"] += sum(len(es) for _, _, es in parts)

    def col(i):
        return T.cols[:, i:i + 1]
    JB, KB, PC, HI, PM, CORR, G8, IL = 0, 2, 4, 5, 7, 8, 9, 10

    mine = [gr for gr in _planes(T, topo) if rank in gr][0]
    me = mine.index(rank)
    nq = len(mine)
    peers = [mine[(me + i) % nq] for i in range(1, nq)]
    eng, home = _engines(T, topo, core)
    ne = len(eng) // nq
    landed = sum(len(es) for s in range(NR) for call in _code_calls(T, topo, s) for _, r, es in call if r == rank)

    dma("a", T.bt[:], T.b[:], "ldb", [], ["bt"])
    dma("s", T.xt[:, 0:512], T.x[:, 0:512], "ldx0", [], ["xt0"])
    dma("s", T.xt[:, 512:1024], T.x[:, 512:1024], "ldx1", [], ["xt1"])
    dma("s", T.wt[:], T.w[:], "ldw", ["xt0", "xt1", "bt"], ["wt"])

    iota(T.dI[:], [[1, 130]], 0, -1, ["dI"])
    iota(T.pint[:, 0:1], [[0, 1]], 0, 1, ["pi0"], small=False)
    iota(col(PC), [[0, 1]], 0, 1, ["pc"])
    iota(T.ik[:], [[1, 128]], 0, 0, ["ik"])
    iota(T.i16[:], [[0, 8], [1, 16]], 0, 0, ["i16"])
    iota(T.Ct[:, 515:1536:4], [[0, 256]], 0, 0, ["Cc"])
    iota(T.Ct[:, 513:1024:4], [[0, 128]], 1, 0, ["Cd"])
    iota(T.Ct[:, 1025:1536:4], [[0, 128]], 0, 0, ["Ce"])
    iota(T.c16[:], [[16, 16]], 0, 0, ["c16"])

    dg = T.dI[:, 0:128]
    fill(T.zer[:], 0.0, ["zer"])
    fill(T.Jt[:], 0.0, ["Jz"])
    afill(T.Ct[:, 0:512:2], 256, -256.0, ["Ca"])
    afill(T.Ct[:, 1:512:2], 256, -1.0, ["Cb"])
    afill(T.Ft[:, 1:512:2], 256, 1.0, ["Fz"])
    afill(T.Mt[:, 512:520:2], 4, 0.0, ["Mz"])
    ts(T.Jt[:, 2:514:4], dg, 0.0, 128.0, A.is_equal, A.mult, ["dI", "Jz"], ["Ja"])
    ts(T.Jt[:, 3:514:4], dg, 0.0, None, A.is_gt, None, ["dI", "Jz"], ["Jb"])
    ts(T.pint[:, 4:5], T.pint[:, 0:1], 15, None, A.bitwise_and, None, ["pi0"], ["pi1"])
    ts(T.nI[:], T.dI[:], 0.0, -1.0, A.is_equal, A.mult, ["dI"], ["nI"])
    op("v", lambda: V.tensor_copy(col(PM), T.pint[:, 4:5]), ["pi1"], ["pm"])
    for h in range(2):
        quant("J", 128 * h, 128 * h + 128, T.Jt[:, 2 - 2 * h:514 - 2 * h], ["Ja", "Jb"], ["J%d" % h])
    act(col(HI), col(PM), ["pm", "pc"], ["hi"], bias=col(PC), scale=-1.0)
    act(T.Ct[:, 512:1024:2], T.Ft[:, 1:512:2], ["pm", "Fz"], ["Cf"], bias=col(PM))
    act(T.Ct[:, 1024:1536:4], T.zer[:, 0:128], ["hi", "zer"], ["Cg"], bias=col(HI))
    act(T.Ct[:, 1026:1536:4], T.Ct[:, 1024:1536:4], ["Cg"], ["Ch"], bias=128.0)

    quant("Bb", 0, 128, T.bt[:], ["bt"], ["Bb"])
    for h in range(2):
        quant("W0", 128 * h, 128 * h + 128, T.xt[:, 512 * h:512 * h + 512], ["xt%d" % h],
              ["W0%dq" % h, "W0%ds" % h])

    def running_max(lo, dst, bank, init, rd, tag):
        op("v", lambda: V.tensor_tensor_scan(dst[:, lo:lo + 128], T["ps%d" % bank][:, 0:128], T.zer[:, 0:128], init,
                                             A.max, A.add), ["ps%d" % bank, "zer"] + rd, [tag])

    def count(lo, n, src, cnt, rd, ctag):
        op("a", lambda: S.activation(T.below[:, 130 * cnt:130 * cnt + n], src[:, lo:lo + n], F.Sign,
                                     bias=src[:, lo + n - 1:lo + n], scale=-1.0, accum_out=col(cnt)), rd, [ctag])

    def latch(lo, bank, plo):
        op("v", lambda: V.tensor_tensor_scan(T.D[:, lo:lo + 128], T.Am[:], T["ps%d" % bank][:, plo:plo + 128], 0.0,
                                             A.add, A.max), ["ps%d" % bank, "Am"], ["D%d" % lo])

    LOW = -1e29
    NI = NR * Q_
    bb, bk = "Bb", ["Bb"]
    for t in range(R_):
        P, L, I, Aq, Bn, W = ["%s%d" % (n, t) for n in "PLIABW"]
        Wn = "W%d" % (t + 1)
        th = [[W + "%dq" % h, W + "%ds" % h] for h in range(2)]
        tw = [W + "0", W + "1"]
        pk = [P + "0q", P + "0s", P + "1q", P + "1s"]
        offa, offb = "offa%d" % t, "offb%d" % t

        for h in range(2):
            mm(4 * h, 128, bb, 0, W, 128 * h, th[h] + bk)
            mm(1 + h, 128, W, 128 * h, bb, 0, th[h] + bk)
        for h in range(2):
            running_max(128 * h, T.R, 4 * h, T.R[:, 127:128] if h else LOW, ["R0"] if h else [], "R%d" % h)
            running_max(128 * h, T.RT, 1 + h, LOW, [], "RT%d" % h)
        count(0, 128, T.R, JB, ["R0"], "jb0")
        count(127, 129, T.R, JB + 1, ["R0", "R1"], "jb1")
        for h in range(2):
            count(128 * h, 128, T.RT, KB + h, ["RT%d" % h], "kb%d" % h)
        if t == 0:
            quant("C", 0, 128, T.Ct[:, 0:512], ["Ca", "Cb"], ["C0"])
        ts(T.Ft[:, 2:512:4], T.ik[:], col(JB + 1), -1.0, A.subtract, A.is_equal, ["ik", "jb1"], ["Ft1"])
        ts(T.Ft[:, 0:512:4], T.ik[:], col(JB), T.below[:, 130:131], A.is_equal, A.is_gt, ["ik", "jb0", "jb1"], ["Ft0"])
        quant("F", 0, 128, T.Ft[:], ["Ft0", "Ft1", "Fz"], ["F"])
        for h in range(2):
            mm(3 + 2 * h, 128, "F", 0, "J", 128 * h, ["F", "J%d" % h])
        if t == 0:
            ts(T.A0[:], T.i16[:], col(PM), DROP + STEP, A.not_equal, A.mult, ["i16", "pm"], ["A0"])
        for h in range(2):
            ts(T.Mt[:, 2 * h:512:4], T["ps%d" % (3 + 2 * h)][:, 0:128], col(KB + h), 128.0, A.subtract, A.is_equal,
               ["ps%d" % (3 + 2 * h), "kb%d" % h], ["Mt%d" % h])
        for h, more in ((0, "zer"), (1, "nI")):
            op("v", lambda: V.tensor_tensor_scan(T.Mt[:, 2 * h + 1:520:4], T.Mt[:, 2 * h:520:4], T[more][:, 0:130],
                                                 0.0, A.add, A.add), ["Mt%d" % h, "Mz", more], ["N%d" % h])
        quant("M", 0, 130, T.Mt[:], ["Mt0", "Mt1", "N0", "N1", "Mz"], ["M"])
        mm(2, 130, "J", 0, "M", 0, ["J0", "M"])
        mm(0, 128, "C", 0, "M", 0, ["C0", "M"])
        if t == 0:
            quant("C", 128, 384, T.Ct[:, 512:1536], ["C" + c for c in "cdefgh"], ["C1"])
            act(T.Am[:], T.A0[:], ["A0"], ["Am"], bias=-DROP)
        mm(6, 128, "C", 256, "M", 0, ["C1", "M"], True, False)
        ts(T.Mt[:, 1:512:4], T.ps0[:, 0:128], T.ps2[:, 128:129], col(PC), A.add, A.is_gt, ["ps0", "ps2", "pc"], ["N0"])
        quant("U", 0, 128, T.Mt[:, 0:512], ["Mt0", "Mt1", "N0", "N1"], ["U"])
        mm(6, 128, "C", 128, "U", 0, ["C1", "U"], False, True)
        if t == 0:
            ts(col(CORR), col(PM), -STEP, 15 * STEP + 1.0, A.mult, A.add, ["pm"], ["corr"])
        latch(0, 6, 0)
        ts(T[offa][:], T.D[:, 15:128:16], col(CORR), None, A.subtract, None, ["D0", "corr"], [offa])
        for h in (1 - 2 * me // nq, 2 * me // nq):
            pick(L, NI + 64 * h, W, 256, offa, 4 * h, 4 * h + 4, tw, P + "%d" % h)

        for i, call in enumerate(_code_calls(T, topo, rank)):
            send([(T[L + "q"][:, NI + Q_ * u:NI + Q_ * u + Q_].bitcast(dt.uint8),
                   [(T.cores[r], T[L + "q"][:, Q_ * rank:Q_ * rank + Q_].bitcast(dt.uint8))], es)
                  for u, r, es in call], "p%d" % t, [P + "%dq" % (2 * u // nq) for u, _, _ in call])
            if i == 0:
                send([(T[L + "s"][:, NI:NI + K_], [(c, T["H%d" % t][:]) for c, _ in _helpers(T, topo, rank)], home)],
                     "h%d" % t, [P + "0s", P + "1s"])

        oq = Q_ // 16
        pick(L, Q_ * rank, W, 256, offa, oq * me, oq * me + oq, tw, L + "o")
        act(T.par[0:1, 128 * t:128 * t + 128], T.ps6[0:1, 0:128], ["ps6"], ["par%d" % t], bias=-1.0)
        if t == 0:
            fill(T.Et[:], 0.0, ["Ez"])
            ts(col(G8), col(PM), float(NR), 1.0 - NI, A.is_ge, A.mult, ["pm"], ["g8"])
            ts(T.Et[:, 3:515:4], dg, 0.0, 0.125, A.is_equal, A.mult, ["dI", "Ez"], ["Et"])
            ts(col(IL), col(PM), float(Q_), col(G8), A.mult, A.add, ["pm", "g8"], ["il"])
            for b in range(4):
                quant("E", 128 * b, 128 * b + 128, T.Et[:, 3 - b:515 - b], ["Et"], ["E%d" % b])
            ts(T.offi[:], T.c16[:], 0.125, col(IL), A.mult, A.add, ["c16", "il"], ["offi"])
            afill(T.msk[:], NI, 1.0, ["msk"])
            afill(T.msk[:, 0:NI:NR], Q_, 0.0, ["msk"])
            for i in (0, 3):
                afill(T.Kt[:, i:1024:4], 256, 0.0, ["Kz%d" % i])
            afill(T.At[:, 256:512], 256, 0.0, ["Az"])
            afill(T.At[:, 4 * Q_:256], 256 - 4 * Q_, 0.0, ["Ay"])
        dma("s", T.pa[t:t + 1, :], T.par[0:1, 128 * t:128 * t + 128], "out", ["par%d" % t], [])
        mm(2, 384, "M", 0, "E", 0, ["M", "E0", "E1", "E2"])
        for h in range(2):
            for slot, size in ((2, 8.0), (1, 1024.0)):
                act(T.Kt[:, 512 * h + slot:512 * h + 512:4], T.ps2[:, 256 * h:256 * h + 128], ["ps2"],
                    ["K%d%d" % (h, slot)], scale=size)
        if t == 0:
            ts(T.j16[:], T.c16[:], col(PM), None, A.add, None, ["c16", "pm"], ["j16"])
            op("v", lambda: V.tensor_copy(T.offo[:], T.j16[:]), ["j16"], ["offo"])
            ts(T.u16[:], T.j16[:], col(CORR), None, A.add, None, ["j16", "corr"], ["u16"])
        quant("K", 0, 256, T.Kt[:], ["K01", "K02", "K11", "K12", "Kz0", "Kz3"], ["K"])
        mm(1, 256, "C", 256, "K", 0, ["C1", "K"], True, False)
        mm(1, 256, "C", 128, "K", 0, ["C1", "K"], False, True)

        arrives("p%d" % t, landed, [L + "q"])
        arrives("s%d" % t, (NR - 1) * ne, [L + "s"])
        ni = 4 if t == 0 else 2
        part = [(I, NI // ni * i, L, NI, "offi", NI // 16 // ni * i, NI // 16 // ni * (i + 1), [L, L + "o"],
                 I + "%d" % i) for i in range(ni)]
        for p in part:
            pick_codes(*p)
        for i, p in enumerate(part):
            pick_scales("v" if t == 0 and i % 2 else "a", *p)
        ik = [[I + "%d%s" % (i, k) for i in range(ni // 2 * h, ni // 2 * (h + 1)) for k in "qs"] for h in range(2)]
        lk = [L + "q", L + "s", L + "oq", L + "os", "E0"] + pk
        bank = {(1, 0): 4, (3, 0): 6, (2, 0): 5, (1, 1): 3, (2, 1): 0, (3, 1): 2}
        for r in range(3):
            mm(7, 128, "E", 0, L, Q_ * r, lk, r == 0, False)
        for (b, h), k in bank.items():
            mm(k, 128, "E", 128 * b, I, 128 * h, ik[h] + ["E%d" % b])
        for r in range(3, NR):
            mm(7, 128, "E", 0, L, Q_ * r, lk, False, r == NR - 1)

        def add_up(lo, n, src, rd, tag):
            op("v", lambda: V.tensor_tensor_scan(T.Z[:, lo:lo + n], T.msk[:, 0:n], src, 0.0, A.mult, A.add),
               rd + ["msk"], [tag])

        def sums(b):
            return T.Z[:, NI * (b - 1) + NR - 1:NI * b:NR]
        for h in range(2):
            for b in (1, 3):
                k = "ps%d" % bank[b, h]
                add_up(NI * (b - 1) + 128 * h, 128, T[k][:, 0:128], [k], "Z%d%d" % (b, h))
        for h in range(2):
            k = "ps%d" % bank[2, h]
            act(T.Zc[:, 128 * h:128 * h + 128], T[k][:, 0:128], [k], ["Zc%d" % h])
        add_up(NI, NI, T.Zc[:], ["Zc0", "Zc1"], "Z2")
        act(T.At[:, 1:4 * Q_:4], sums(1), ["Z10", "Z11"], ["At1"])
        act(T.At[:, 3:4 * Q_:4], sums(3), ["Z30", "Z31"], ["At3"])
        act(T.At[:, 0:4 * Q_:4], T.ps7[:, 0:Q_], ["ps7"], ["At0"])
        op("v", lambda: V.tensor_copy(T.At[:, 2:4 * Q_:4], sums(2)), ["Z2"], ["At2"])
        quant(Aq, 0, 128, T.At[:], ["At0", "At1", "At2", "At3", "Az", "Ay"], [Aq + "q", Aq + "s"])
        for kind in "qs":
            src = T[Aq + kind][:, 0:Q_]
            dst = T[Bn + kind][:, Q_ * me:Q_ * me + Q_]
            if kind == "q":
                src, dst = src.bitcast(dt.uint8), dst.bitcast(dt.uint8)
            send([(src, [(T.cores[r], dst) for r in peers], eng)], "b%d" % t, [Aq + kind])
        arrives("b%d" % t, (nq - 1) * 2 * len(eng), [Bn])

        for b in range(4):
            mm(4 + b, 128, "E", 128 * b, L, NI, ["E%d" % b] + pk, True, False)
        pick(Bn, Q_ * me, Aq, 128, "offo", 0, oq, [Aq], Bn + "o")
        latch(0, 1, 0)
        latch(128, 1, 128)
        if t == 0:
            quant("Ww", 0, 128, T.wt[:], ["wt"], ["Ww"])
        op("v", lambda: V.tensor_tensor(T.z16[:], T.D[:, 15:256:16], T.u16[:], A.max), ["D0", "D128", "u16"], ["z16"])
        ts(T[offb][:], T.z16[:], col(CORR), None, A.subtract, None, ["z16", "corr"], [offb])

        bb, bk = Bn, [Bn, Bn + "oq", Bn + "os"]
        for b in range(4):
            mm(4 + b, 128, "E", 128 * b, bb, 0, ["E%d" % b] + bk, False, True)
        last = t == R_ - 1
        if last:
            mm(0, 128, "Ww", 0, bb, 0, ["Ww"] + bk)
        for b in range(4):
            src = T["ps%d" % (4 + b)][:, 0:128]
            if b % 2 == 1:
                ts(T.Vt[:, b:512:4], src, 4.0, None, A.mult, None, ["ps%d" % (4 + b)], ["Vt%d" % b])
            else:
                act(T.Vt[:, b:512:4], src, ["ps%d" % (4 + b)], ["Vt%d" % b], scale=4.0)
        if last:
            act(T.ysb[:, 256:384], T.ps0[:, 0:128], ["ps0"], ["yb"])
            dma("s", T.y[:, 256:384], T.ysb[:, 256:384], "out", ["yb"], [])
        quant(W, 256, 384, T.Vt[:], ["Vt0", "Vt1", "Vt2", "Vt3"], [W + "bq", W + "bs"])
        for h in range(2):
            pick(Wn, 128 * h, W, 384, offb, 8 * h, 8 * h + 8, tw + [W + "b"], Wn + "%d" % h)

    tb = "W%d" % R_

    def scales_out(q, k):
        dma(q, T.osc[4 * k:4 * k + 4, :], T[tb + "s"][32 * k:32 * k + 4, :], "out", [tb + "0s", tb + "1s"], [])
    for h in range(2):
        mm(1 + h, 128, "Ww", 0, tb, 128 * h, ["Ww", tb + "%dq" % h, tb + "%ds" % h])
        dma("s", T.oc[:, 512 * h:512 * h + 512], T[tb + "q"][:, 128 * h:128 * h + 128].bitcast(dt.uint8), "out",
            [tb + "%dq" % h], [])
    scales_out("a", 3)
    for k in range(3):
        scales_out("s", k)
    for h in range(2):
        op("v", lambda: V.tensor_copy(T.ysb[:, 128 * h:128 * h + 128], T["ps%d" % (1 + h)][:, 0:128]),
           ["ps%d" % (1 + h)], ["y%d" % h])
        dma("a", T.y[:, 128 * h:128 * h + 128], T.ysb[:, 128 * h:128 * h + 128], "out", ["y%d" % h], [])

    for s in SEMAPHORES:
        if total[s]:
            g.wait_ge(T.sem[s], total[s])
